import numpy as np, ml_dtypes
CORES = [242,247,114,119]
N = 4
T, CAPP = 512, 256
def entries(a): return a.T.reshape(-1)
def pack(v, P): return np.ascontiguousarray(np.asarray(v, np.int32).reshape(-1, P).T)
def places(p):
    n = len(p); pl = [-1] * n; c = int(np.setdiff1d(np.arange(n), p[p != np.arange(n)])[:1].sum()); q = p.tolist()
    for k in range(n):
        if pl[c] >= 0: break
        pl[c] = k; c = q[c]
    return np.array(pl, np.int64)
def most(p):
    c = np.bincount(np.arange(N * T) // T * N + places(p) // T, minlength=N * N).reshape(N, N); return int((c - np.diag(np.diag(c))).max())
def deal(rng, m): return np.argsort(rng.random((N, m)), axis=1)
def lists(rng, how):
    n, i, G = N * T, np.arange(N), T // CAPP
    if how == "order": o = np.arange(n)
    elif how == "stride": o = np.lexsort((rng.random(n), np.arange(n) % 8))
    elif how == "mixed":
        a, t, m = rng.permutation(N), int(rng.integers(1, CAPP)), N - 1; z = a[m]; L = np.zeros((N, N), np.int64)
        for s in range(1, G + 1): L[a[:m], a[(i[:m] + s) % m]] = CAPP
        L[z, z], L[a[0], a[1]], L[a[0], z], L[z, a[1]] = T - t, CAPP - t, t, t
        lo, hi = np.zeros((N, N), np.int64), np.where(np.eye(N) > 0, T - CAPP, CAPP); lo[z, z], hi[z, z], lo[a[1], a[2]] = T - CAPP + 1, T - 1, CAPP
        for k in range(4 * N * N):
            r, u, d, v = np.append(rng.permutation(N)[:2], rng.permutation(N)[:2])
            t = int(rng.integers(0, 1 + min(hi[r, d] - L[r, d], hi[u, v] - L[u, v], L[r, v] - lo[r, v], L[u, d] - lo[u, d])))
            L[r, d] += t; L[u, v] += t; L[r, v] -= t; L[u, d] -= t
        o = np.lexsort((rng.random(n), np.concatenate([rng.permutation(np.repeat(i, l)) for l in L])))
    else:
        g, j = np.arange(G)[:, None], np.arange(CAPP)
        s = {"back": np.append(1 + np.arange(G - 1), N - 1), "full": 1 + np.arange(G), "hops": 1 + (G + np.arange(G)) % (N - 1)}[how]
        to = (i[:, None] + s) % N
        c, Q = deal(rng, T).reshape(N, G, CAPP), deal(rng, T).reshape(N, G, CAPP)
        if how == "hops": Q[:] = G * j + g
        if how == "back":
            c = np.sort(np.concatenate([np.full((N, 1), T - 1), 1 + deal(rng, T - 2), np.zeros((N, 1), np.int64)], axis=1).reshape(N, G, CAPP), axis=2); Q[:] = CAPP * g + j[::-1]
        o = np.empty(n, np.int64); o[T * to[:, :, None] + Q[to, g.T]] = T * i[:, None, None] + c
    p = np.empty(n, np.int64); p[o[:-1]] = o[1:]; p[o[-1]] = o[-1]
    return {"nx": np.stack([pack(v, 16) for v in p.reshape(N, T)])}
def setup_inputs(rng):
    return dict({"x": rng.standard_normal((N, 128, T), dtype=np.float32).astype(ml_dtypes.bfloat16)}, **lists(rng, "mixed"))
def setup_inputs_back(rng):
    d = setup_inputs(rng); d.update(lists(rng, "back"))
    for k in ("x",): d[k] = (d[k].astype(np.float32) * 1048576.0).astype(d[k].dtype)
    return d
def setup_inputs_full(rng):
    d = setup_inputs(rng); d.update(lists(rng, "full"))
    for k in ("x",): d[k] = (d[k].astype(np.float32) * (1 / 1024.0)).astype(d[k].dtype)
    return d
def setup_inputs_hops(rng):
    d = setup_inputs(rng); d.update(lists(rng, "hops"))
    return d
def setup_inputs_order(rng):
    d = setup_inputs(rng); d.update(lists(rng, "order"))
    return d
def setup_inputs_stride(rng):
    d = setup_inputs(rng); d.update(lists(rng, "stride"))
    return d
def check_inputs(x):
    bad = []
    if x["nx"].min() < 0 or x["nx"].max() >= N * T: bad.append("nx out of range")
    if bad: return bad
    p = np.concatenate([entries(a) for a in x["nx"]])
    if (p == np.arange(N * T)).sum() != 1: bad.append("not exactly one column names itself")
    if not np.array_equal(np.sort(places(p)), np.arange(N * T)): bad.append("the line does not run through all columns, each once")
    elif most(p) > CAPP: bad.append("more than CAPP columns go from one rank's x to another rank's y")
    return bad
def reference(x, nx):
    X = np.concatenate(list(x), axis=1); p = np.concatenate([entries(a) for a in nx])
    pl = places(p); Y = np.zeros_like(X); Y[:, pl] = X
    return {"y": np.stack([Y[:, T * r:T * r + T] for r in range(N)])}

@@ -1,0 +1,283 @@
+from concourse.bass import DstId, RemoteDMATransfer
+from concourse.mybir import AluOpType as A, AxisListType, ActivationFunctionType as F
+
+BF, FL = "bfloat16", "float32"
+SCRATCH = {
+    "nxs": ("sbuf", [128, 64], "int32"),
+    "xw": ("sbuf", [128, 2048], BF),
+    "yo": ("sbuf", [128, 512], BF),
+    "pi": ("sbuf", [128, 1], "int32"), "v16": ("sbuf", [128, 16], "int32"),
+    "ju": ("sbuf", [128, 128], BF), "jg": ("sbuf", [128, 128], BF), "jq": ("sbuf", [128, 128], BF),
+    "jj": ("sbuf", [128, 256], BF), "jv": ("sbuf", [128, 64], BF), "je": ("sbuf", [128, 64], BF),
+    "pc": ("sbuf", [128, 16], "int32"), "pf": ("sbuf", [128, 16], FL), "pd": ("sbuf", [128, 32], FL),
+    "l16": ("sbuf", [128, 2], "uint16"), "lz": ("sbuf", [128, 16], "uint16"),
+    "i0": ("sbuf", [128, 16], FL), "q3b": ("sbuf", [128, 16], FL),
+    "mu": ("sbuf", [128, 256], BF), "cs": ("sbuf", [128, 256], BF),
+    "bd": ("sbuf", [128, 128], BF), "lx": ("sbuf", [128, 128], BF), "lr": ("sbuf", [128, 128], BF),
+    "ca": ("sbuf", [128, 128], BF), "cb": ("sbuf", [128, 128], BF), "cc": ("sbuf", [128, 128], BF),
+    "cd": ("sbuf", [128, 128], BF), "ce": ("sbuf", [128, 128], BF), "cf": ("sbuf", [128, 128], BF),
+    "lw": ("sbuf", [128, 128], BF), "lwt": ("sbuf", [128, 128], BF), "lwh": ("sbuf", [128, 128], BF),
+    "ones": ("sbuf", [128, 128], FL), "ef": ("sbuf", [128, 64], BF), "zm": ("sbuf", [128, 64], BF),
+    "n0": ("sbuf", [128, 16], "int32"), "t0": ("sbuf", [128, 16], "int32"), "h0": ("sbuf", [128, 16], "int32"),
+    "e0": ("sbuf", [128, 16], FL), "e1": ("sbuf", [128, 16], FL), "e2": ("sbuf", [128, 16], FL),
+    "er": ("sbuf", [128, 1], FL), "hd": ("sbuf", [128, 4], "int32"), "hf": ("sbuf", [128, 1], FL),
+    "zt": ("sbuf", [128, 256], BF), "zh": ("sbuf", [128, 256], BF),
+    "w0": ("sbuf", [128, 512], BF), "w1": ("sbuf", [128, 512], BF),
+    "m": ("sbuf", [128, 320], BF), "gt": ("sbuf", [128, 320], BF), "sc": ("sbuf", [128, 320], FL),
+    "off": ("sbuf", [128, 20], "uint16"), "zf": ("sbuf", [128, 64], BF), "offy": ("sbuf", [128, 32], "uint16"),
+    "pxa": ("psum", [128, 512], FL), "pxb": ("psum", [128, 512], FL), "pwa": ("psum", [128, 512], FL),
+    "pwb": ("psum", [128, 512], FL), "pra": ("psum", [128, 512], FL), "prb": ("psum", [128, 512], FL),
+    "ps": ("psum", [128, 512], FL), "pt": ("psum", [128, 512], FL),
+}
+SEMAPHORES = ["sv", "ss", "sp", "si", "dn", "dx", "dy", "rl", "an", "ax"]
+
+
+def bits(m):
+    return [1 << k for k in range(32) if m >> k & 1]
+
+
+def shares(core, dests, topo):
+    out, used, by = {}, 0, {}
+    for d in dests:
+        by.setdefault(topo.mask(core, d), []).append(d)
+    for m in sorted(by, key=lambda v: len(bits(v))):
+        free, n = bits(m & ~used), 1
+        while n * 2 * len(by[m]) <= len(free):
+            n *= 2
+        for k, d in enumerate(by[m]):
+            out[d] = sum(free[k * n:k * n + n])
+            used |= out[d]
+    return out
+
+
+def rank_program(g, core, T, topo):
+    rank = T.rank_of(core)
+    if rank is None:
+        return
+    sem = T.sem
+    others = [d for d in T.cores if d != core]
+    Q = {"v": g.vector, "s": g.scalar, "p": g.tensor, "i": g, "y": g.sync}
+    S = {"v": "sv", "s": "ss", "p": "sp", "i": "si"}
+    cnt, seen = {}, {}
+
+    def wait(q, deps):
+        need = {}
+        for d in deps:
+            need[d[0]] = max(need.get(d[0], 0), d[1])
+        for s in sorted(need):
+            if seen.get((q, s), 0) < need[s]:
+                Q[q].wait_ge(sem[s], need[s])
+                seen[(q, s)] = need[s]
+
+    def op(q, call, deps=()):
+        wait(q, deps)
+        call(Q[q]).then_inc(sem[S[q]], 1)
+        cnt[S[q]] = cnt.get(S[q], 0) + 1
+        return (S[q], cnt[S[q]])
+
+    def V(call, *deps):
+        return op("v", call, deps)
+
+    def TS(out, in0, s1, s2, o1, o2, *deps):
+        if o2 is None:
+            return V(lambda e: e.tensor_scalar(out, in0, s1, None, o1), *deps)
+        return V(lambda e: e.tensor_scalar(out, in0, s1, s2, o1, o2), *deps)
+
+    def TT(out, a, b, o, *deps):
+        return V(lambda e: e.tensor_tensor(out, a, b, o), *deps)
+
+    def CP(out, a, *deps):
+        return V(lambda e: e.tensor_copy(out, a), *deps)
+
+    def MM(out, l, r, a, z, *deps):
+        return op("p", lambda e: e.matmul(out, l, r, a, z), deps)
+
+    def ACT(out, a, f, b, *deps):
+        return op("s", lambda e: e.activation(out, a, f, bias=b), deps)
+
+    c0 = 16 * rank
+    slot = T.nxs[:, c0:c0 + 16]
+    p0 = 32 * rank
+    g.sync.dma_start(T.nxs[p0:p0 + 16, c0:c0 + 16], T.nx[:, 0:16]).then_inc(sem.dn, 16)
+    g.scalar.dma_start(T.nxs[p0 + 16:p0 + 32, c0:c0 + 16], T.nx[:, 16:32]).then_inc(sem.dn, 16)
+    g.sync.dma_start(T.xw[:, 512 * rank:512 * rank + 512], T.x[:, :]).then_inc(sem.dx, 16)
+    ms = []
+    for a, b in {0: [(32, 64), (64, 128)], 1: [(0, 32), (64, 128)], 2: [(0, 64), (96, 128)], 3: [(0, 64), (64, 96)]}[rank]:
+        ms.append(V(lambda e: e.memset(T.nxs[a:b, c0:c0 + 16], 0)))
+    V(lambda e: e.memset(T.ones[:], 1.0))
+
+    def IO(out, pat, base=0, cm=0, flag=True):
+        if flag:
+            return op("i", lambda e: e.iota(out, pat, base, cm, allow_small_or_imprecise_dtypes=True))
+        return op("i", lambda e: e.iota(out, pat, base, cm))
+    i_p = IO(T.pi[:], [[0, 1]], 0, 1, False)
+    i_v = IO(T.v16[:], [[1, 16]], 0, 0, False)
+    i_u = IO(T.ju[:], [[0, 8], [1, 16]])
+    i_g = IO(T.jg[:], [[1, 8], [0, 16]])
+    i_q = IO(T.jq[:], [[0, 8], [1, 8], [8, 2]])
+    mk = shares(core, others, topo)
+
+    def send(ap, rs):
+        tr = []
+        for d in others:
+            rid, pid = topo.addr(d, core)
+            tr.append(RemoteDMATransfer(dst_ids=[DstId(rid=rid, pnc=pid)], dma_engine_mask=mk[d], remote_sem=rs, src=ap, dst=ap))
+        g.remote_dma_fused(tr, local_sem=sem.rl)
+    wait("i", [("dn", 32)] + ms)
+    send(slot, sem.an)
+    i_j = IO(T.jj[:], [[1, 256]], -128)
+    i_7 = IO(T.jv[:], [[0, 8], [1, 8]])
+    i_e = IO(T.je[:], [[0, 2], [1, 4], [0, 8]])
+    wait("i", [("dx", 16)])
+    send(T.xw[:, 512 * rank:512 * rank + 512], sem.ax)
+    arrive = sum(len(bits(shares(d, [e for e in T.cores if e != d], topo)[core])) for d in others)
+
+    pc, pf, pd = T.pc, T.pf, T.pd
+    for k, ops in enumerate([(0, 15), (4, 15), (1, 7), (0, 1), (0, 240), (1, 112)]):
+        c_ = TS(pc[:, k:k + 1], T.pi[:], ops[0], ops[1], A.logical_shift_right, A.bitwise_and, i_p)
+    c_f = CP(pf[:, 0:6], pc[:, 0:6], c_)
+    u, gc, q3, ch = pf[:, 0:1], pf[:, 1:2], pf[:, 2:3], pf[:, 3:4]
+
+    def D(k):
+        return pd[:, k:k + 1]
+    TS(T.l16[:, 0:1], pf[:, 5:6], u, None, A.add, None, c_f)
+    CP(T.lz[:], T.v16[:], i_v)
+    TS(D(7), gc, 7.0, None, A.is_equal, None)
+    TS(D(5), ch, -1.0, 1.0, A.mult, A.add)
+    c_a = TS(D(13), ch, 8.0, gc, A.mult, A.add)
+    c_b = TS(D(6), D(7), -8.0, gc, A.mult, A.add, c_a)
+    TS(D(8), D(7), 1.0, -0.5, A.mult, A.add)
+    TS(D(14), gc, 8.0, None, A.add, None)
+    c_b = TS(D(18), D(6), 1.0, None, A.add, None, c_b)
+    TS(T.mu[:, 0:128], T.ju[:], u, None, A.is_equal, None, i_u)
+    TS(T.mu[:, 128:256], T.ju[:], u, None, A.is_equal, None)
+    c_c = TS(D(15), D(18), 8.0, None, A.add, None, c_b)
+    TS(D(16), ch, 8.0, D(18), A.mult, A.add)
+    TS(T.bd[:], T.jg[:], gc, None, A.is_equal, None, i_g)
+    TS(T.ca[:], T.jq[:], D(14), 0.5, A.is_equal, A.mult, i_q)
+    c_1 = TS(T.cb[:], T.jq[:], D(15), D(8), A.is_equal, A.mult, c_c)
+    TS(T.cc[:], T.jq[:], gc, 0.5, A.is_equal, A.mult)
+    c_2 = TS(T.cd[:], T.jq[:], D(18), D(8), A.is_equal, A.mult)
+    TT(T.lwh[:], T.ca[:], T.cb[:], A.add, c_1)
+    TT(T.lwt[:], T.cc[:], T.cd[:], A.add, c_2)
+    TS(D(2), q3, -1.0, 0.5, A.mult, A.add)
+    TS(D(11), q3, -256.0, 2096128.5, A.mult, A.add)
+    TS(D(4), u, 0.0, -128.0, A.is_equal, A.mult)
+    c_e = TS(D(10), pf[:, 4:5], 16.0, u, A.mult, A.add)
+    TS(T.ce[:], T.jq[:], D(13), 0.5, A.is_equal, A.mult)
+    c_3 = TS(T.cf[:], T.jq[:], D(16), D(8), A.is_equal, A.mult)
+    TS(T.i0[:], T.v16[:], 16.0, D(10), A.mult, A.add, c_e)
+    TS(T.q3b[:], T.v16[:], 0.0, D(11), A.mult, A.add)
+    TT(T.lw[:], T.ce[:], T.cf[:], A.add, c_3)
+    TS(T.lx[:], T.jg[:], gc, D(5), A.is_equal, A.mult)
+    TS(T.lr[:], T.jg[:], gc, ch, A.is_equal, A.mult)
+    TS(T.cs[:], T.mu[:], -16640.0, 256.0, A.mult, A.add)
+    TS(D(0), u, 256.0, -3712.0, A.mult, A.add)
+    TS(D(1), u, 256.0, -3456.0, A.mult, A.add)
+    TS(D(3), u, 0.0, None, A.is_equal, None)
+    c_9 = TS(D(9), u, 1.0, 3.0, A.is_equal, A.mult)
+    for k in range(7):
+        c_ = TS(pc[:, 6 + k:7 + k], T.pi[:], k, 1, A.logical_shift_right, A.bitwise_and)
+    TS(D(17), ch, 0.5, D(9), A.mult, A.add, c_9)
+    c_f = CP(pf[:, 6:13], pc[:, 6:13], c_)
+    TS(pd[:, 20:27], pf[:, 6:13], -256.0, D(1), A.mult, A.add, c_f)
+    c_w = TS(D(19), pf[:, 6:7], -256.0, 256.0, A.mult, A.add)
+    TS(T.w0[:, 256:512], T.jj[:], D(3), D(17), A.mult, A.add, i_j, c_w)
+    TS(T.w1[:, 256:512], T.jj[:], D(3), D(17), A.mult, A.add)
+    TS(T.ef[:, 0:32], T.jv[:, 0:32], gc, D(5), A.is_equal, A.mult, i_7)
+    TS(T.ef[:, 32:64], T.jv[:, 32:64], gc, ch, A.is_equal, A.mult)
+    TS(T.zm[:, 0:32], T.je[:, 0:32], gc, None, A.is_equal, None, i_e)
+    c_z = TS(T.zm[:, 32:64], T.je[:, 32:64], gc, 256.0, A.is_equal, A.mult)
+
+    wait("v", [("dn", 32), ("an", arrive), c_z])
+    n_0 = CP(T.n0[:], T.nxs[:].indirect(T.l16[:, 0:1]))
+    a_h = TS(T.h0[:], T.n0[:], 8, None, A.logical_shift_right, None, n_0)
+    a_t = TS(T.t0[:], T.n0[:], 255, None, A.bitwise_and, None)
+    z_h = TT(T.zh[:], T.h0[:].indirect(T.lz[:]), T.mu[:], A.mult, a_h)
+    z_a = TT(T.zt[:, 0:128], T.t0[:].indirect(T.lz[:, 0:8]), T.mu[:, 0:128], A.mult, a_t)
+    z_b = TT(T.zt[:, 128:256], T.t0[:].indirect(T.lz[:, 8:16]), T.mu[:, 128:256], A.mult)
+    MM(T.pwa[:, 0:128], T.lwh[:], T.zh[:, 0:128], True, False, z_h)
+    MM(T.pwb[:, 0:128], T.lwh[:], T.zh[:, 128:256], True, False)
+    r_b = MM(T.pra[:, 0:128], T.bd[:], T.zh[:, 0:128], True, True)
+    w_0 = MM(T.pwa[:, 0:128], T.lwt[:], T.zt[:, 0:128], False, True, z_a)
+    w_1 = MM(T.pwb[:, 0:128], T.lwt[:], T.zt[:, 128:256], False, True, z_b)
+    m_a = ACT(T.m[:, 0:128], T.pra[:, 0:128], F.Sign, D(2), r_b)
+    w_ev = [ACT(T.w0[:, 0:128], T.pwa[:, 0:128], F.Identity, D(4), w_0),
+            ACT(T.w0[:, 128:256], T.pwb[:, 0:128], F.Identity, D(4), w_1)]
+    h_1 = TT(T.e0[:], T.n0[:], T.i0[:], A.is_equal)
+    o_ab = CP(T.off[:, 0:16], T.t0[:], a_t)
+    h_2 = TT(T.e1[:], T.e0[:], T.i0[:], A.mult, h_1)
+    h_3 = TT(T.e2[:], T.e1[:], T.n0[:], A.subtract, h_2)
+    h_4 = V(lambda e: e.tensor_reduce(T.er[:], T.e2[:], AxisListType.X, A.add), h_3)
+    h_5 = MM(T.ps[:, 0:1], T.ones[:], T.er[:], True, True, h_4)
+    r_b = MM(T.prb[:, 0:128], T.bd[:], T.zh[:, 128:256], True, True)
+    h_6 = ACT(T.hf[:], T.ps[:, 0:1], F.Copy, 0.0, h_5)
+    m_s = ACT(T.m[:, 256:272], T.q3b[:], F.Sign, T.hf[:], h_6)
+    m_b = ACT(T.m[:, 128:256], T.prb[:, 0:128], F.Sign, D(2), r_b)
+
+    wins = [T.w0, T.w1]
+    last = {0: 9, 1: 9, 2: 10, 3: 10}[rank]
+    o_s = None
+    for k in range(last):
+        cur, nxt = wins[k % 2], wins[(k + 1) % 2]
+        square = k < (8 if rank == 0 else last)
+        ns = {7: 16, 8: 32, 9: 64 if rank == 3 else 0}.get(k, 16)
+        so = {7: 17, 8: 18}.get(k, 16)
+        nk, lo, nb = ns // 16, 128, 128 + ns
+        sm = D(20 + k + 1) if k + 1 <= 6 else D(0)
+        if square:
+            g_a = TT(T.gt[:, 0:128], cur[:].indirect(T.off[:, 0:8]), T.m[:, 0:128], A.mult, o_ab, m_a, *w_ev)
+            if k == 0:
+                h_7 = TS(T.hd[:, 0:1], T.hf[:], 2096128.0, None, A.add, None, h_6)
+                h_8 = TS(T.hd[:, 1:2], T.hd[:, 0:1], 255, None, A.bitwise_and, None, h_7)
+                o_s = TS(T.off[:, 16:17], T.hd[:, 1:2], D(19), None, A.add, None, h_8)
+            g_b = TT(T.gt[:, 128:128 + nb], cur[:].indirect(T.off[:, 8:8 + nb // 16]), T.m[:, 128:128 + nb], A.mult,
+                     m_b, o_s, m_s)
+            x_a = MM(T.pxa[:, 0:128], T.lx[:], T.gt[:, 0:128], True, True, g_a)
+            r_a = MM(T.pra[:, 0:128], T.lr[:], T.gt[:, 0:128], True, True)
+            x_b = MM(T.pxb[:, 0:nb], T.lx[:], T.gt[:, 128:128 + nb], True, True, g_b)
+            w_a = MM(T.pwa[:, 0:128], T.lw[:], T.gt[:, 0:128], True, True)
+            w_b = MM(T.pwb[:, 0:64], T.lw[:], T.gt[:, 128:192], True, True)
+            w_c = MM(T.pt[:, 0:64], T.lw[:], T.gt[:, 192:256], True, True)
+            r_b = MM(T.prb[:, 0:nb], T.lr[:], T.gt[:, 128:128 + nb], True, True)
+            m_a = ACT(T.m[:, 0:128], T.pra[:, 0:128], F.Sign, D(2), r_a)
+            w_ev = [ACT(nxt[:, 0:128], T.pwa[:, 0:128], F.Copy, 0.0, w_a),
+                    ACT(nxt[:, 128:192], T.pwb[:, 0:64], F.Copy, 0.0, w_b)]
+            if ns and so == 16:
+                m_b = m_s = ACT(T.m[:, 128:128 + nb], T.prb[:, 0:nb], F.Sign, D(2), r_b)
+            else:
+                m_b = ACT(T.m[:, 128:256], T.prb[:, 0:128], F.Sign, D(2), r_b)
+            s_a = V(lambda e: e.tensor_tensor_scan(T.sc[:, 0:128], T.cs[:, 0:128], T.pxa[:, 0:128], 0.0, A.add, A.max), x_a)
+        else:
+            lo, nb = 0, ns
+            g_b = TT(T.gt[:, 256:256 + ns], cur[:].indirect(T.off[:, 16:16 + nk]), T.m[:, 256:256 + ns], A.mult,
+                     o_s, m_s, *w_ev)
+            x_b = MM(T.pxb[:, 0:nb], T.lx[:], T.gt[:, 256:256 + ns], True, True, g_b)
+            r_b = MM(T.prb[:, 0:nb], T.lr[:], T.gt[:, 256:256 + ns], True, True)
+        if ns and (so != 16 or not square):
+            m_s = ACT(T.m[:, 16 * so:16 * so + ns], T.prb[:, lo:lo + ns], F.Sign, D(2), r_b)
+        s_b = V(lambda e: e.tensor_tensor_scan(T.sc[:, 256 - lo:256 - lo + nb], T.cs[:, 0:nb], T.pxb[:, 0:nb], 0.0, A.add, A.max), x_b)
+        if square:
+            o_ab = TS(T.off[:, 0:16], T.sc[:, 15:256:16], D(0), None, A.add, None, s_b)
+        if ns:
+            o_s = TS(T.off[:, so:so + nk], T.sc[:, 256 + 15:256 + 16 * nk:16], sm, None, A.add, None, s_b)
+        if square:
+            w_ev.append(CP(nxt[:, 192:256], T.pt[:, 0:64], w_c))
+
+    win = wins[0][:, 256:512] if rank == 0 else wins[last % 2][:, 0:256]
+    g_f = TT(T.gt[:, 256:320], win.indirect(T.off[:, 16:20]), T.m[:, 256:320], A.mult, o_s, m_s, *w_ev)
+    f_1 = MM(T.ps[0:64, 0:64], T.gt[:, 256:320], T.ef[:], True, True, g_f)
+    f_2 = TT(T.zf[0:64, :], T.ps[0:64, 0:64], T.zm[0:64, :], A.mult, f_1)
+    MM(T.pt[:, 0:32], T.mu[0:64, 0:128], T.zf[0:64, 0:32], True, False, f_2)
+    f_3 = MM(T.pt[:, 0:32], T.mu[0:64, 0:128], T.zf[0:64, 32:64], False, True)
+    f_4 = TS(T.offy[:], T.pt[:, 0:32], 128.0, None, A.add, None, f_3)
+    ready = [f_4, ("ax", arrive), ("dx", 16)]
+    y_a = CP(T.yo[:, 0:256], T.xw[:].indirect(T.offy[:, 0:16]), *ready)
+    y_b = ACT(T.yo[:, 256:512], T.xw[:].indirect(T.offy[:, 16:32]), F.Identity, -0.0, *ready)
+    wait("y", [y_a])
+    g.sync.dma_start(T.y[:, 0:256], T.yo[:, 0:256]).then_inc(sem.dy, 16)
+    wait("s", [y_b])
+    g.scalar.dma_start(T.y[:, 256:512], T.yo[:, 256:512]).then_inc(sem.dy, 16)
+    sent = 2 * sum(len(bits(mk[d])) for d in others)
+    wait("i", [("rl", sent), ("sv", cnt["sv"]), ("ss", cnt["ss"]), ("sp", cnt["sp"]), ("dy", 32)])
+    wait("v", [("si", cnt["si"])])

@@ -1,5 +1,5 @@
 from concourse.bass import DstId, RemoteDMATransfer
-from concourse.mybir import AluOpType as A, AxisListType, ActivationFunctionType as F
+from concourse.mybir import AluOpType as A, ActivationFunctionType as F
 
 BF, FL = "bfloat16", "float32"
 SCRATCH = {
@@ -17,10 +17,11 @@ SCRATCH = {
     "ca": ("sbuf", [128, 128], BF), "cb": ("sbuf", [128, 128], BF), "cc": ("sbuf", [128, 128], BF),
     "cd": ("sbuf", [128, 128], BF), "ce": ("sbuf", [128, 128], BF), "cf": ("sbuf", [128, 128], BF),
     "lw": ("sbuf", [128, 128], BF), "lwt": ("sbuf", [128, 128], BF), "lwh": ("sbuf", [128, 128], BF),
-    "ones": ("sbuf", [128, 128], FL), "ef": ("sbuf", [128, 64], BF), "zm": ("sbuf", [128, 64], BF),
+    "on1": ("sbuf", [128, 128], BF), "on2": ("sbuf", [128, 128], BF),
+    "ef": ("sbuf", [128, 64], BF), "zm": ("sbuf", [128, 64], BF),
     "n0": ("sbuf", [128, 16], "int32"), "t0": ("sbuf", [128, 16], "int32"), "h0": ("sbuf", [128, 16], "int32"),
-    "e0": ("sbuf", [128, 16], FL), "e1": ("sbuf", [128, 16], FL), "e2": ("sbuf", [128, 16], FL),
-    "er": ("sbuf", [128, 1], FL), "hd": ("sbuf", [128, 4], "int32"), "hf": ("sbuf", [128, 1], FL),
+    "e0": ("sbuf", [128, 16], FL), "e1": ("sbuf", [128, 16], BF), "e2": ("sbuf", [128, 16], BF),
+    "er": ("sbuf", [128, 16], FL), "hd": ("sbuf", [128, 4], "int32"), "hf": ("sbuf", [128, 1], FL),
     "zt": ("sbuf", [128, 256], BF), "zh": ("sbuf", [128, 256], BF),
     "w0": ("sbuf", [128, 512], BF), "w1": ("sbuf", [128, 512], BF),
     "m": ("sbuf", [128, 320], BF), "gt": ("sbuf", [128, 320], BF), "sc": ("sbuf", [128, 320], FL),
@@ -37,13 +38,13 @@ def bits(m):
 
 
 def shares(core, dests, topo):
-    out, used, by = {}, 0, {}
+    out, used, by, n = {}, 0, {}, 16
     for d in dests:
         by.setdefault(topo.mask(core, d), []).append(d)
     for m in sorted(by, key=lambda v: len(bits(v))):
-        free, n = bits(m & ~used), 1
-        while n * 2 * len(by[m]) <= len(free):
-            n *= 2
+        free = bits(m & ~used)
+        while n * len(by[m]) > len(free):
+            n //= 2
         for k, d in enumerate(by[m]):
             out[d] = sum(free[k * n:k * n + n])
             used |= out[d]
@@ -89,11 +90,17 @@ def rank_program(g, core, T, topo):
     def CP(out, a, *deps):
         return V(lambda e: e.tensor_copy(out, a), *deps)
 
+    def SCAN(out, c, x, *deps):
+        return V(lambda e: e.tensor_tensor_scan(out, c, x, 0.0, A.add, A.max), *deps)
+
     def MM(out, l, r, a, z, *deps):
         return op("p", lambda e: e.matmul(out, l, r, a, z), deps)
 
     def ACT(out, a, f, b, *deps):
         return op("s", lambda e: e.activation(out, a, f, bias=b), deps)
+
+    def LIN(out, a, m, b, *deps):
+        return op("s", lambda e: e.activation(out, a, F.Identity, bias=b, scale=m), deps)
 
     c0 = 16 * rank
     slot = T.nxs[:, c0:c0 + 16]
@@ -104,7 +111,6 @@ def rank_program(g, core, T, topo):
     ms = []
     for a, b in {0: [(32, 64), (64, 128)], 1: [(0, 32), (64, 128)], 2: [(0, 64), (96, 128)], 3: [(0, 64), (64, 96)]}[rank]:
         ms.append(V(lambda e: e.memset(T.nxs[a:b, c0:c0 + 16], 0)))
-    V(lambda e: e.memset(T.ones[:], 1.0))
 
     def IO(out, pat, base=0, cm=0, flag=True):
         if flag:
@@ -140,99 +146,100 @@ def rank_program(g, core, T, topo):
 
     def D(k):
         return pd[:, k:k + 1]
-    TS(T.l16[:, 0:1], pf[:, 5:6], u, None, A.add, None, c_f)
     CP(T.lz[:], T.v16[:], i_v)
-    TS(D(7), gc, 7.0, None, A.is_equal, None)
-    TS(D(5), ch, -1.0, 1.0, A.mult, A.add)
-    c_a = TS(D(13), ch, 8.0, gc, A.mult, A.add)
-    c_b = TS(D(6), D(7), -8.0, gc, A.mult, A.add, c_a)
-    TS(D(8), D(7), 1.0, -0.5, A.mult, A.add)
-    TS(D(14), gc, 8.0, None, A.add, None)
-    c_b = TS(D(18), D(6), 1.0, None, A.add, None, c_b)
+    c_7 = TS(D(7), gc, 7.0, None, A.is_equal, None, c_f)
+    TS(T.l16[:, 0:1], pf[:, 5:6], u, None, A.add, None)
+    c_b = TS(D(6), D(7), -8.0, gc, A.mult, A.add, c_7)
     TS(T.mu[:, 0:128], T.ju[:], u, None, A.is_equal, None, i_u)
-    TS(T.mu[:, 128:256], T.ju[:], u, None, A.is_equal, None)
-    c_c = TS(D(15), D(18), 8.0, None, A.add, None, c_b)
-    TS(D(16), ch, 8.0, D(18), A.mult, A.add)
+    c_b = TS(D(18), D(6), 1.0, None, A.add, None, c_b)
+    c_u = TS(T.mu[:, 128:256], T.ju[:], u, None, A.is_equal, None)
+    k_8 = LIN(D(8), D(7), 1.0, -0.5, c_7)
+    k_e = LIN(D(14), gc, 1.0, 8.0)
+    k_f = LIN(D(15), D(18), 1.0, 8.0, c_b)
+    k_g = LIN(D(16), ch, 8.0, D(18))
+    k_d = LIN(D(13), ch, 8.0, gc)
+    k_5 = LIN(D(5), ch, -1.0, 1.0)
+    LIN(D(2), q3, -1.0, 0.5)
+    k_b = LIN(D(11), q3, -256.0, 2096128.5)
+    k_a = LIN(D(10), pf[:, 4:5], 16.0, u)
+    LIN(D(0), u, 256.0, -3712.0)
+    k_1 = LIN(D(1), u, 256.0, -3456.0)
+    LIN(T.i0[:], T.ju[:, 0:16], 16.0, D(10), i_u, k_a)
+    k_q = LIN(T.q3b[:], T.ju[:, 0:16], 0.0, D(11), k_b)
+    LIN(T.cs[:], T.mu[:], -16640.0, 256.0, c_u)
     TS(T.bd[:], T.jg[:], gc, None, A.is_equal, None, i_g)
-    TS(T.ca[:], T.jq[:], D(14), 0.5, A.is_equal, A.mult, i_q)
-    c_1 = TS(T.cb[:], T.jq[:], D(15), D(8), A.is_equal, A.mult, c_c)
-    TS(T.cc[:], T.jq[:], gc, 0.5, A.is_equal, A.mult)
-    c_2 = TS(T.cd[:], T.jq[:], D(18), D(8), A.is_equal, A.mult)
-    TT(T.lwh[:], T.ca[:], T.cb[:], A.add, c_1)
+    TS(T.cc[:], T.jq[:], gc, 0.5, A.is_equal, A.mult, i_q)
+    TS(T.ca[:], T.jq[:], D(14), 0.5, A.is_equal, A.mult, k_e)
+    c_2 = TS(T.cd[:], T.jq[:], D(18), D(8), A.is_equal, A.mult, k_8, c_b)
+    c_1 = TS(T.cb[:], T.jq[:], D(15), D(8), A.is_equal, A.mult, k_f)
     TT(T.lwt[:], T.cc[:], T.cd[:], A.add, c_2)
-    TS(D(2), q3, -1.0, 0.5, A.mult, A.add)
-    TS(D(11), q3, -256.0, 2096128.5, A.mult, A.add)
+    TT(T.lwh[:], T.ca[:], T.cb[:], A.add, c_1)
     TS(D(4), u, 0.0, -128.0, A.is_equal, A.mult)
-    c_e = TS(D(10), pf[:, 4:5], 16.0, u, A.mult, A.add)
-    TS(T.ce[:], T.jq[:], D(13), 0.5, A.is_equal, A.mult)
-    c_3 = TS(T.cf[:], T.jq[:], D(16), D(8), A.is_equal, A.mult)
-    TS(T.i0[:], T.v16[:], 16.0, D(10), A.mult, A.add, c_e)
-    TS(T.q3b[:], T.v16[:], 0.0, D(11), A.mult, A.add)
+    V(lambda e: e.memset(T.on1[:], -1.0))
+    V(lambda e: e.memset(T.on2[:], -256.0))
+    TS(T.ce[:], T.jq[:], D(13), 0.5, A.is_equal, A.mult, k_d)
+    c_3 = TS(T.cf[:], T.jq[:], D(16), D(8), A.is_equal, A.mult, k_g)
+    TS(T.lx[:], T.jg[:], gc, D(5), A.is_equal, A.mult, k_5)
     TT(T.lw[:], T.ce[:], T.cf[:], A.add, c_3)
-    TS(T.lx[:], T.jg[:], gc, D(5), A.is_equal, A.mult)
     TS(T.lr[:], T.jg[:], gc, ch, A.is_equal, A.mult)
-    TS(T.cs[:], T.mu[:], -16640.0, 256.0, A.mult, A.add)
-    TS(D(0), u, 256.0, -3712.0, A.mult, A.add)
-    TS(D(1), u, 256.0, -3456.0, A.mult, A.add)
-    TS(D(3), u, 0.0, None, A.is_equal, None)
     c_9 = TS(D(9), u, 1.0, 3.0, A.is_equal, A.mult)
+    c_3 = TS(D(3), u, 0.0, None, A.is_equal, None)
+    k_h = LIN(D(17), ch, 0.5, D(9), c_9)
+    idw = [LIN(w[:, 256:512], T.jj[:], D(3), D(17), i_j, k_h, c_3) for w in (T.w0, T.w1)]
     for k in range(7):
         c_ = TS(pc[:, 6 + k:7 + k], T.pi[:], k, 1, A.logical_shift_right, A.bitwise_and)
-    TS(D(17), ch, 0.5, D(9), A.mult, A.add, c_9)
     c_f = CP(pf[:, 6:13], pc[:, 6:13], c_)
-    TS(pd[:, 20:27], pf[:, 6:13], -256.0, D(1), A.mult, A.add, c_f)
-    c_w = TS(D(19), pf[:, 6:7], -256.0, 256.0, A.mult, A.add)
-    TS(T.w0[:, 256:512], T.jj[:], D(3), D(17), A.mult, A.add, i_j, c_w)
-    TS(T.w1[:, 256:512], T.jj[:], D(3), D(17), A.mult, A.add)
-    TS(T.ef[:, 0:32], T.jv[:, 0:32], gc, D(5), A.is_equal, A.mult, i_7)
-    TS(T.ef[:, 32:64], T.jv[:, 32:64], gc, ch, A.is_equal, A.mult)
-    TS(T.zm[:, 0:32], T.je[:, 0:32], gc, None, A.is_equal, None, i_e)
-    c_z = TS(T.zm[:, 32:64], T.je[:, 32:64], gc, 256.0, A.is_equal, A.mult)
+    TS(D(19), pf[:, 6:7], -256.0, 256.0, A.mult, A.add, c_f)
+    TS(pd[:, 20:27], pf[:, 6:13], -256.0, D(1), A.mult, A.add, k_1)
+    extra = [lambda: TS(T.ef[:, 0:32], T.jv[:, 0:32], gc, D(5), A.is_equal, A.mult, i_7),
+             lambda: TS(T.ef[:, 32:64], T.jv[:, 32:64], gc, ch, A.is_equal, A.mult),
+             lambda: TS(T.zm[:, 0:32], T.je[:, 0:32], gc, None, A.is_equal, None, i_e),
+             lambda: TS(T.zm[:, 32:64], T.je[:, 32:64], gc, 256.0, A.is_equal, A.mult)]
 
-    wait("v", [("dn", 32), ("an", arrive), c_z])
+    wait("v", [("dn", 32), ("an", arrive), ("sv", cnt["sv"]), k_q])
     n_0 = CP(T.n0[:], T.nxs[:].indirect(T.l16[:, 0:1]))
     a_h = TS(T.h0[:], T.n0[:], 8, None, A.logical_shift_right, None, n_0)
     a_t = TS(T.t0[:], T.n0[:], 255, None, A.bitwise_and, None)
+    h_1 = TT(T.e0[:], T.n0[:], T.i0[:], A.not_equal)
     z_h = TT(T.zh[:], T.h0[:].indirect(T.lz[:]), T.mu[:], A.mult, a_h)
-    z_a = TT(T.zt[:, 0:128], T.t0[:].indirect(T.lz[:, 0:8]), T.mu[:, 0:128], A.mult, a_t)
+    TT(T.e1[:], T.e0[:], T.t0[:], A.mult, a_t, h_1)
+    h_2 = TT(T.e2[:], T.e0[:], T.h0[:], A.mult)
+    z_a = TT(T.zt[:, 0:128], T.t0[:].indirect(T.lz[:, 0:8]), T.mu[:, 0:128], A.mult)
     z_b = TT(T.zt[:, 128:256], T.t0[:].indirect(T.lz[:, 8:16]), T.mu[:, 128:256], A.mult)
+    o_ab = CP(T.off[:, 0:16], T.t0[:])
     MM(T.pwa[:, 0:128], T.lwh[:], T.zh[:, 0:128], True, False, z_h)
+    MM(T.ps[:, 0:16], T.on1[:], T.e1[:], True, False, h_2)
+    h_5 = MM(T.ps[:, 0:16], T.on2[:], T.e2[:], False, True)
     MM(T.pwb[:, 0:128], T.lwh[:], T.zh[:, 128:256], True, False)
-    r_b = MM(T.pra[:, 0:128], T.bd[:], T.zh[:, 0:128], True, True)
+    r_a = MM(T.pra[:, 0:128], T.bd[:], T.zh[:, 0:128], True, True)
     w_0 = MM(T.pwa[:, 0:128], T.lwt[:], T.zt[:, 0:128], False, True, z_a)
     w_1 = MM(T.pwb[:, 0:128], T.lwt[:], T.zt[:, 128:256], False, True, z_b)
-    m_a = ACT(T.m[:, 0:128], T.pra[:, 0:128], F.Sign, D(2), r_b)
-    w_ev = [ACT(T.w0[:, 0:128], T.pwa[:, 0:128], F.Identity, D(4), w_0),
-            ACT(T.w0[:, 128:256], T.pwb[:, 0:128], F.Identity, D(4), w_1)]
-    h_1 = TT(T.e0[:], T.n0[:], T.i0[:], A.is_equal)
-    o_ab = CP(T.off[:, 0:16], T.t0[:], a_t)
-    h_2 = TT(T.e1[:], T.e0[:], T.i0[:], A.mult, h_1)
-    h_3 = TT(T.e2[:], T.e1[:], T.n0[:], A.subtract, h_2)
-    h_4 = V(lambda e: e.tensor_reduce(T.er[:], T.e2[:], AxisListType.X, A.add), h_3)
-    h_5 = MM(T.ps[:, 0:1], T.ones[:], T.er[:], True, True, h_4)
     r_b = MM(T.prb[:, 0:128], T.bd[:], T.zh[:, 128:256], True, True)
-    h_6 = ACT(T.hf[:], T.ps[:, 0:1], F.Copy, 0.0, h_5)
+    h_6 = op("s", lambda e: e.activation(T.er[:], T.ps[:, 0:16], F.Copy, accum_out=T.hf[:]), [h_5])
+    m_a = ACT(T.m[:, 0:128], T.pra[:, 0:128], F.Sign, D(2), r_a)
     m_s = ACT(T.m[:, 256:272], T.q3b[:], F.Sign, T.hf[:], h_6)
+    w_ev = [ACT(T.w0[:, 0:128], T.pwa[:, 0:128], F.Identity, D(4), w_0)]
     m_b = ACT(T.m[:, 128:256], T.prb[:, 0:128], F.Sign, D(2), r_b)
+    h_7 = TS(T.hd[:, 0:1], T.hf[:], 2096128.0, None, A.add, None, h_6)
+    w_ev.append(TS(T.w0[:, 128:256], T.pwb[:, 0:128], D(4), None, A.add, None, w_1))
+    h_8 = TS(T.hd[:, 1:2], T.hd[:, 0:1], 255, None, A.bitwise_and, None, h_7)
+    o_s = TS(T.off[:, 16:17], T.hd[:, 1:2], D(19), None, A.add, None, h_8)
 
     wins = [T.w0, T.w1]
     last = {0: 9, 1: 9, 2: 10, 3: 10}[rank]
-    o_s = None
+    lastsq = 7 if rank == 0 else last - 1
     for k in range(last):
         cur, nxt = wins[k % 2], wins[(k + 1) % 2]
-        square = k < (8 if rank == 0 else last)
+        square = k < lastsq
         ns = {7: 16, 8: 32, 9: 64 if rank == 3 else 0}.get(k, 16)
         so = {7: 17, 8: 18}.get(k, 16)
         nk, lo, nb = ns // 16, 128, 128 + ns
         sm = D(20 + k + 1) if k + 1 <= 6 else D(0)
-        if square:
+        if k <= lastsq:
             g_a = TT(T.gt[:, 0:128], cur[:].indirect(T.off[:, 0:8]), T.m[:, 0:128], A.mult, o_ab, m_a, *w_ev)
-            if k == 0:
-                h_7 = TS(T.hd[:, 0:1], T.hf[:], 2096128.0, None, A.add, None, h_6)
-                h_8 = TS(T.hd[:, 1:2], T.hd[:, 0:1], 255, None, A.bitwise_and, None, h_7)
-                o_s = TS(T.off[:, 16:17], T.hd[:, 1:2], D(19), None, A.add, None, h_8)
             g_b = TT(T.gt[:, 128:128 + nb], cur[:].indirect(T.off[:, 8:8 + nb // 16]), T.m[:, 128:128 + nb], A.mult,
-                     m_b, o_s, m_s)
+                     m_b, o_s, m_s, *idw)
+        if square:
             x_a = MM(T.pxa[:, 0:128], T.lx[:], T.gt[:, 0:128], True, True, g_a)
             r_a = MM(T.pra[:, 0:128], T.lr[:], T.gt[:, 0:128], True, True)
             x_b = MM(T.pxb[:, 0:nb], T.lx[:], T.gt[:, 128:128 + nb], True, True, g_b)
@@ -247,7 +254,20 @@ def rank_program(g, core, T, topo):
                 m_b = m_s = ACT(T.m[:, 128:128 + nb], T.prb[:, 0:nb], F.Sign, D(2), r_b)
             else:
                 m_b = ACT(T.m[:, 128:256], T.prb[:, 0:128], F.Sign, D(2), r_b)
-            s_a = V(lambda e: e.tensor_tensor_scan(T.sc[:, 0:128], T.cs[:, 0:128], T.pxa[:, 0:128], 0.0, A.add, A.max), x_a)
+            s_a = SCAN(T.sc[:, 0:128], T.cs[:, 0:128], T.pxa[:, 0:128], x_a)
+            if 2 <= k < 6:
+                extra[k - 2]()
+        elif k == lastsq:
+            lo, nb = 0, ns
+            w_a = MM(T.pwa[:, 0:128], T.lw[:], T.gt[:, 0:128], True, True, g_a)
+            if ns:
+                x_b = MM(T.pxb[:, 0:nb], T.lx[:], T.gt[:, 256:256 + ns], True, True, g_b)
+            w_b = MM(T.pwb[:, 0:64], T.lw[:], T.gt[:, 128:192], True, True, g_b)
+            w_c = MM(T.pt[:, 0:64], T.lw[:], T.gt[:, 192:256], True, True)
+            if ns:
+                r_b = MM(T.prb[:, 0:nb], T.lr[:], T.gt[:, 256:256 + ns], True, True)
+            w_ev = [ACT(nxt[:, 0:128], T.pwa[:, 0:128], F.Copy, 0.0, w_a),
+                    ACT(nxt[:, 128:192], T.pwb[:, 0:64], F.Copy, 0.0, w_b)]
         else:
             lo, nb = 0, ns
             g_b = TT(T.gt[:, 256:256 + ns], cur[:].indirect(T.off[:, 16:16 + nk]), T.m[:, 256:256 + ns], A.mult,
@@ -256,13 +276,14 @@ def rank_program(g, core, T, topo):
             r_b = MM(T.prb[:, 0:nb], T.lr[:], T.gt[:, 256:256 + ns], True, True)
         if ns and (so != 16 or not square):
             m_s = ACT(T.m[:, 16 * so:16 * so + ns], T.prb[:, lo:lo + ns], F.Sign, D(2), r_b)
-        s_b = V(lambda e: e.tensor_tensor_scan(T.sc[:, 256 - lo:256 - lo + nb], T.cs[:, 0:nb], T.pxb[:, 0:nb], 0.0, A.add, A.max), x_b)
+        if nb:
+            s_b = SCAN(T.sc[:, 256 - lo:256 - lo + nb], T.cs[:, 0:nb], T.pxb[:, 0:nb], x_b)
         if square:
             o_ab = TS(T.off[:, 0:16], T.sc[:, 15:256:16], D(0), None, A.add, None, s_b)
+        if k <= lastsq:
+            w_ev.append(CP(nxt[:, 192:256], T.pt[:, 0:64], w_c))
         if ns:
             o_s = TS(T.off[:, so:so + nk], T.sc[:, 256 + 15:256 + 16 * nk:16], sm, None, A.add, None, s_b)
-        if square:
-            w_ev.append(CP(nxt[:, 192:256], T.pt[:, 0:64], w_c))
 
     win = wins[0][:, 256:512] if rank == 0 else wins[last % 2][:, 0:256]
     g_f = TT(T.gt[:, 256:320], win.indirect(T.off[:, 16:20]), T.m[:, 256:320], A.mult, o_s, m_s, *w_ev)

@@ -19,18 +19,19 @@ SCRATCH = {
     "lw": ("sbuf", [128, 128], BF), "lwt": ("sbuf", [128, 128], BF), "lwh": ("sbuf", [128, 128], BF),
     "on1": ("sbuf", [128, 128], BF), "on2": ("sbuf", [128, 128], BF),
     "ef": ("sbuf", [128, 64], BF), "zm": ("sbuf", [128, 64], BF),
-    "n0": ("sbuf", [128, 16], "int32"), "t0": ("sbuf", [128, 16], "int32"), "h0": ("sbuf", [128, 16], "int32"),
+    "t0": ("sbuf", [128, 16], "int32"), "h0": ("sbuf", [128, 16], "int32"),
     "e0": ("sbuf", [128, 16], FL), "e1": ("sbuf", [128, 16], BF), "e2": ("sbuf", [128, 16], BF),
     "er": ("sbuf", [128, 16], FL), "hd": ("sbuf", [128, 4], "int32"), "hf": ("sbuf", [128, 1], FL),
     "zt": ("sbuf", [128, 256], BF), "zh": ("sbuf", [128, 256], BF),
     "w0": ("sbuf", [128, 512], BF), "w1": ("sbuf", [128, 512], BF),
     "m": ("sbuf", [128, 320], BF), "gt": ("sbuf", [128, 320], BF), "sc": ("sbuf", [128, 320], FL),
     "off": ("sbuf", [128, 20], "uint16"), "zf": ("sbuf", [128, 64], BF), "offy": ("sbuf", [128, 32], "uint16"),
-    "pxa": ("psum", [128, 512], FL), "pxb": ("psum", [128, 512], FL), "pwa": ("psum", [128, 512], FL),
-    "pwb": ("psum", [128, 512], FL), "pra": ("psum", [128, 512], FL), "prb": ("psum", [128, 512], FL),
-    "ps": ("psum", [128, 512], FL), "pt": ("psum", [128, 512], FL),
+    "px0": ("psum", [128, 512], FL), "px1": ("psum", [128, 512], FL), "px2": ("psum", [128, 512], FL),
+    "pw0": ("psum", [128, 512], FL), "pw1": ("psum", [128, 512], FL), "pw2": ("psum", [128, 512], FL),
+    "pr1": ("psum", [128, 512], FL), "pr2": ("psum", [128, 512], FL),
 }
-SEMAPHORES = ["sv", "ss", "sp", "si", "dn", "dx", "dy", "rl", "an", "ax"]
+SEMAPHORES = ["sv", "ss", "sp", "si", "dn", "dx", "dy", "rl", "an", "ax", "ap"]
+SZ = [64, 128, 64]
 
 
 def bits(m):
@@ -57,6 +58,8 @@ def rank_program(g, core, T, topo):
         return
     sem = T.sem
     others = [d for d in T.cores if d != core]
+    near = [d for d in others if topo.host(d) == topo.host(core) and topo.chip(d) == topo.chip(core)][0]
+    peer = [d for d in others if topo.same_plane(core, d) and topo.die(d) == topo.die(core)][0]
     Q = {"v": g.vector, "s": g.scalar, "p": g.tensor, "i": g, "y": g.sync}
     S = {"v": "sv", "s": "ss", "p": "sp", "i": "si"}
     cnt, seen = {}, {}
@@ -121,22 +124,36 @@ def rank_program(g, core, T, topo):
     i_u = IO(T.ju[:], [[0, 8], [1, 16]])
     i_g = IO(T.jg[:], [[1, 8], [0, 16]])
     i_q = IO(T.jq[:], [[0, 8], [1, 8], [8, 2]])
-    mk = shares(core, others, topo)
+    sent = [0]
 
-    def send(ap, rs):
-        tr = []
-        for d in others:
+    def send(dests, ap):
+        mk, tr = shares(core, [d for d, _ in dests], topo), []
+        for d, r_ in dests:
             rid, pid = topo.addr(d, core)
-            tr.append(RemoteDMATransfer(dst_ids=[DstId(rid=rid, pnc=pid)], dma_engine_mask=mk[d], remote_sem=rs, src=ap, dst=ap))
+            tr.append(RemoteDMATransfer(dst_ids=[DstId(rid=rid, pnc=pid)], dma_engine_mask=mk[d], remote_sem=r_, src=ap, dst=ap))
+            sent[0] += len(bits(mk[d]))
         g.remote_dma_fused(tr, local_sem=sem.rl)
+
+    def part(src, dests, d):
+        return len(bits(shares(src, dests, topo)[d]))
+
+    def xs(c):
+        r_ = T.rank_of(c)
+        return T.xw[:, 512 * r_:512 * r_ + 512]
     wait("i", [("dn", 32)] + ms)
-    send(slot, sem.an)
+    send([(d, sem.an) for d in others], slot)
     i_j = IO(T.jj[:], [[1, 256]], -128)
+    wait("i", [("dx", 16)])
+    send([(near, sem.ax), (peer, sem.ap)], xs(core))
     i_7 = IO(T.jv[:], [[0, 8], [1, 8]])
     i_e = IO(T.je[:], [[0, 2], [1, 4], [0, 8]])
-    wait("i", [("dx", 16)])
-    send(T.xw[:, 512 * rank:512 * rank + 512], sem.ax)
-    arrive = sum(len(bits(shares(d, [e for e in T.cores if e != d], topo)[core])) for d in others)
+    nearpeer = [d for d in others if d not in (near, peer)][0]
+    n_an = sum(part(d, [e for e in T.cores if e != d], core) for d in others)
+    n_ap = part(peer, [nearpeer, core], core)
+    n_ax = part(near, [core, nearpeer], core) + part(near, [core], core)
+    ready = [("ax", n_ax), ("ap", n_ap), ("dx", 16)]
+    wait("i", [("ap", n_ap)])
+    send([(near, sem.ax)], xs(peer))
 
     pc, pf, pd = T.pc, T.pf, T.pd
     for k, ops in enumerate([(0, 15), (4, 15), (1, 7), (0, 1), (0, 240), (1, 112)]):
@@ -196,36 +213,40 @@ def rank_program(g, core, T, topo):
              lambda: TS(T.zm[:, 0:32], T.je[:, 0:32], gc, None, A.is_equal, None, i_e),
              lambda: TS(T.zm[:, 32:64], T.je[:, 32:64], gc, 256.0, A.is_equal, A.mult)]
 
-    wait("v", [("dn", 32), ("an", arrive), ("sv", cnt["sv"]), k_q])
-    n_0 = CP(T.n0[:], T.nxs[:].indirect(T.l16[:, 0:1]))
-    a_h = TS(T.h0[:], T.n0[:], 8, None, A.logical_shift_right, None, n_0)
-    a_t = TS(T.t0[:], T.n0[:], 255, None, A.bitwise_and, None)
-    h_1 = TT(T.e0[:], T.n0[:], T.i0[:], A.not_equal)
+    wait("v", [("dn", 32), ("an", n_an), ("sv", cnt["sv"]), k_q])
+    nx = T.nxs[:].indirect(T.l16[:, 0:1])
+    a_h = TS(T.h0[:], nx, 8, None, A.logical_shift_right, None)
+    a_t = TS(T.t0[:], nx, 255, None, A.bitwise_and, None)
+    h_1 = TT(T.e0[:], nx, T.i0[:], A.not_equal)
     z_h = TT(T.zh[:], T.h0[:].indirect(T.lz[:]), T.mu[:], A.mult, a_h)
     TT(T.e1[:], T.e0[:], T.t0[:], A.mult, a_t, h_1)
     h_2 = TT(T.e2[:], T.e0[:], T.h0[:], A.mult)
-    z_a = TT(T.zt[:, 0:128], T.t0[:].indirect(T.lz[:, 0:8]), T.mu[:, 0:128], A.mult)
-    z_b = TT(T.zt[:, 128:256], T.t0[:].indirect(T.lz[:, 8:16]), T.mu[:, 128:256], A.mult)
-    o_ab = CP(T.off[:, 0:16], T.t0[:])
-    MM(T.pwa[:, 0:128], T.lwh[:], T.zh[:, 0:128], True, False, z_h)
-    MM(T.ps[:, 0:16], T.on1[:], T.e1[:], True, False, h_2)
-    h_5 = MM(T.ps[:, 0:16], T.on2[:], T.e2[:], False, True)
-    MM(T.pwb[:, 0:128], T.lwh[:], T.zh[:, 128:256], True, False)
-    r_a = MM(T.pra[:, 0:128], T.bd[:], T.zh[:, 0:128], True, True)
-    w_0 = MM(T.pwa[:, 0:128], T.lwt[:], T.zt[:, 0:128], False, True, z_a)
-    w_1 = MM(T.pwb[:, 0:128], T.lwt[:], T.zt[:, 128:256], False, True, z_b)
-    r_b = MM(T.prb[:, 0:128], T.bd[:], T.zh[:, 128:256], True, True)
-    h_6 = op("s", lambda e: e.activation(T.er[:], T.ps[:, 0:16], F.Copy, accum_out=T.hf[:]), [h_5])
-    m_a = ACT(T.m[:, 0:128], T.pra[:, 0:128], F.Sign, D(2), r_a)
+    z_a = TT(T.zt[:, 0:192], T.t0[:].indirect(T.lz[:, 0:12]), T.mu[:, 0:192], A.mult)
+    z_b = TT(T.zt[:, 192:256], T.t0[:].indirect(T.lz[:, 12:16]), T.mu[:, 192:256], A.mult)
+    o_t = CP(T.off[:, 0:16], T.t0[:])
+    MM(T.pw0[:, 0:192], T.lwh[:], T.zh[:, 0:192], True, False, z_h)
+    MM(T.pr2[:, 0:16], T.on1[:], T.e1[:], True, False, h_2)
+    h_5 = MM(T.pr2[:, 0:16], T.on2[:], T.e2[:], False, True)
+    MM(T.pw1[:, 0:64], T.lwh[:], T.zh[:, 192:256], True, False)
+    r_a = MM(T.px0[:, 0:64], T.bd[:], T.zh[:, 0:64], True, True)
+    w_0 = MM(T.pw0[:, 0:192], T.lwt[:], T.zt[:, 0:192], False, True, z_a)
+    w_1 = MM(T.pw1[:, 0:64], T.lwt[:], T.zt[:, 192:256], False, True, z_b)
+    r_b = MM(T.pr1[:, 0:192], T.bd[:], T.zh[:, 64:256], True, True)
+    h_6 = op("s", lambda e: e.activation(T.er[:], T.pr2[:, 0:16], F.Copy, accum_out=T.hf[:]), [h_5])
+    m_a = ACT(T.m[:, 0:64], T.px0[:, 0:64], F.Sign, D(2), r_a)
     m_s = ACT(T.m[:, 256:272], T.q3b[:], F.Sign, T.hf[:], h_6)
-    w_ev = [ACT(T.w0[:, 0:128], T.pwa[:, 0:128], F.Identity, D(4), w_0)]
-    m_b = ACT(T.m[:, 128:256], T.prb[:, 0:128], F.Sign, D(2), r_b)
+    w_ev = [ACT(T.w0[:, 0:192], T.pw0[:, 0:192], F.Identity, D(4), w_0)]
+    m_b = ACT(T.m[:, 64:256], T.pr1[:, 0:192], F.Sign, D(2), r_b)
     h_7 = TS(T.hd[:, 0:1], T.hf[:], 2096128.0, None, A.add, None, h_6)
-    w_ev.append(TS(T.w0[:, 128:256], T.pwb[:, 0:128], D(4), None, A.add, None, w_1))
+    w_ev.append(TS(T.w0[:, 192:256], T.pw1[:, 0:64], D(4), None, A.add, None, w_1))
     h_8 = TS(T.hd[:, 1:2], T.hd[:, 0:1], 255, None, A.bitwise_and, None, h_7)
     o_s = TS(T.off[:, 16:17], T.hd[:, 1:2], D(19), None, A.add, None, h_8)
 
     wins = [T.w0, T.w1]
+    px, pw, pr = [T.px0, T.px1, T.px2], [T.pw0, T.pw1, T.pw2], [T.pw0, T.pr1, T.pr2]
+    ST = [0, SZ[0], SZ[0] + SZ[1]]
+    RO = [SZ[0], 0, 0]
+    m_p, o_p = [m_a, m_b, m_b], [o_t, o_t, o_t]
     last = {0: 9, 1: 9, 2: 10, 3: 10}[rank]
     lastsq = 7 if rank == 0 else last - 1
     for k in range(last):
@@ -233,72 +254,83 @@ def rank_program(g, core, T, topo):
         square = k < lastsq
         ns = {7: 16, 8: 32, 9: 64 if rank == 3 else 0}.get(k, 16)
         so = {7: 17, 8: 18}.get(k, 16)
-        nk, lo, nb = ns // 16, 128, 128 + ns
+        nk = ns // 16
+        wd = [SZ[0], SZ[1], SZ[2] + ns]
         sm = D(20 + k + 1) if k + 1 <= 6 else D(0)
+        gg = []
         if k <= lastsq:
-            g_a = TT(T.gt[:, 0:128], cur[:].indirect(T.off[:, 0:8]), T.m[:, 0:128], A.mult, o_ab, m_a, *w_ev)
-            g_b = TT(T.gt[:, 128:128 + nb], cur[:].indirect(T.off[:, 8:8 + nb // 16]), T.m[:, 128:128 + nb], A.mult,
-                     m_b, o_s, m_s, *idw)
+            for i in range(3):
+                a, b = ST[i], ST[i] + wd[i]
+                dep = [o_p[i], m_p[i]] + w_ev + ([o_s, m_s] + idw if i == 2 else [])
+                gg.append(TT(T.gt[:, a:b], cur[:].indirect(T.off[:, a // 16:b // 16]), T.m[:, a:b], A.mult, *dep))
+        else:
+            gg = [None, None, TT(T.gt[:, 256:256 + ns], cur[:].indirect(T.off[:, 16:16 + nk]), T.m[:, 256:256 + ns],
+                                 A.mult, o_s, m_s, *w_ev)]
+
+        def X(i):
+            return MM(px[i][:, 0:wd[i]], T.lx[:], T.gt[:, ST[i]:ST[i] + wd[i]], True, True, gg[i])
+
+        def R(i):
+            return MM(pr[i][:, RO[i]:RO[i] + wd[i]], T.lr[:], T.gt[:, ST[i]:ST[i] + wd[i]], True, True, gg[i])
+
+        def W(i):
+            return MM(pw[i][:, 0:SZ[i]], T.lw[:], T.gt[:, ST[i]:ST[i] + SZ[i]], True, True, gg[i])
+
+        def WE(i, dep):
+            return ACT(nxt[:, ST[i]:ST[i] + SZ[i]], pw[i][:, 0:SZ[i]], F.Copy, 0.0, dep)
+
+        def ME(i, n, dep):
+            return ACT(T.m[:, ST[i]:ST[i] + n], pr[i][:, RO[i]:RO[i] + n], F.Sign, D(2), dep)
+
+        def SC(i, dep):
+            return SCAN(T.sc[:, ST[i]:ST[i] + wd[i]], T.cs[:, 0:wd[i]], px[i][:, 0:wd[i]], dep)
         if square:
-            x_a = MM(T.pxa[:, 0:128], T.lx[:], T.gt[:, 0:128], True, True, g_a)
-            r_a = MM(T.pra[:, 0:128], T.lr[:], T.gt[:, 0:128], True, True)
-            x_b = MM(T.pxb[:, 0:nb], T.lx[:], T.gt[:, 128:128 + nb], True, True, g_b)
-            w_a = MM(T.pwa[:, 0:128], T.lw[:], T.gt[:, 0:128], True, True)
-            w_b = MM(T.pwb[:, 0:64], T.lw[:], T.gt[:, 128:192], True, True)
-            w_c = MM(T.pt[:, 0:64], T.lw[:], T.gt[:, 192:256], True, True)
-            r_b = MM(T.prb[:, 0:nb], T.lr[:], T.gt[:, 128:128 + nb], True, True)
-            m_a = ACT(T.m[:, 0:128], T.pra[:, 0:128], F.Sign, D(2), r_a)
-            w_ev = [ACT(nxt[:, 0:128], T.pwa[:, 0:128], F.Copy, 0.0, w_a),
-                    ACT(nxt[:, 128:192], T.pwb[:, 0:64], F.Copy, 0.0, w_b)]
-            if ns and so == 16:
-                m_b = m_s = ACT(T.m[:, 128:128 + nb], T.prb[:, 0:nb], F.Sign, D(2), r_b)
+            x_0, _, v_0 = X(0), R(0), W(0)
+            x_1, v_1 = X(1), W(1)
+            x_2, v_2 = X(2), W(2)
+            r_1, r_2 = R(1), R(2)
+            m_0 = ME(0, SZ[0], v_0)
+            w_ev = [WE(0, v_0), WE(1, v_1), WE(2, v_2)]
+            m_p = [m_0, ME(1, SZ[1], r_1), ME(2, wd[2] if so == 16 else SZ[2], r_2)]
+            if so == 16:
+                m_s = m_p[2]
             else:
-                m_b = ACT(T.m[:, 128:256], T.prb[:, 0:128], F.Sign, D(2), r_b)
-            s_a = SCAN(T.sc[:, 0:128], T.cs[:, 0:128], T.pxa[:, 0:128], x_a)
+                m_s = ACT(T.m[:, 16 * so:16 * so + ns], T.pr2[:, SZ[2]:wd[2]], F.Sign, D(2), r_2)
+            SC(0, x_0)
             if 2 <= k < 6:
                 extra[k - 2]()
-        elif k == lastsq:
-            lo, nb = 0, ns
-            w_a = MM(T.pwa[:, 0:128], T.lw[:], T.gt[:, 0:128], True, True, g_a)
-            if ns:
-                x_b = MM(T.pxb[:, 0:nb], T.lx[:], T.gt[:, 256:256 + ns], True, True, g_b)
-            w_b = MM(T.pwb[:, 0:64], T.lw[:], T.gt[:, 128:192], True, True, g_b)
-            w_c = MM(T.pt[:, 0:64], T.lw[:], T.gt[:, 192:256], True, True)
-            if ns:
-                r_b = MM(T.prb[:, 0:nb], T.lr[:], T.gt[:, 256:256 + ns], True, True)
-            w_ev = [ACT(nxt[:, 0:128], T.pwa[:, 0:128], F.Copy, 0.0, w_a),
-                    ACT(nxt[:, 128:192], T.pwb[:, 0:64], F.Copy, 0.0, w_b)]
-        else:
-            lo, nb = 0, ns
-            g_b = TT(T.gt[:, 256:256 + ns], cur[:].indirect(T.off[:, 16:16 + nk]), T.m[:, 256:256 + ns], A.mult,
-                     o_s, m_s, *w_ev)
-            x_b = MM(T.pxb[:, 0:nb], T.lx[:], T.gt[:, 256:256 + ns], True, True, g_b)
-            r_b = MM(T.prb[:, 0:nb], T.lr[:], T.gt[:, 256:256 + ns], True, True)
-        if ns and (so != 16 or not square):
-            m_s = ACT(T.m[:, 16 * so:16 * so + ns], T.prb[:, lo:lo + ns], F.Sign, D(2), r_b)
-        if nb:
-            s_b = SCAN(T.sc[:, 256 - lo:256 - lo + nb], T.cs[:, 0:nb], T.pxb[:, 0:nb], x_b)
-        if square:
-            o_ab = TS(T.off[:, 0:16], T.sc[:, 15:256:16], D(0), None, A.add, None, s_b)
-        if k <= lastsq:
-            w_ev.append(CP(nxt[:, 192:256], T.pt[:, 0:64], w_c))
+            s_1 = SC(1, x_1)
+            s_2 = SC(2, x_2)
+            o_1 = TS(T.off[:, 0:ST[2] // 16], T.sc[:, 15:ST[2]:16], D(0), None, A.add, None, s_1)
+            o_p = [o_1, o_1, TS(T.off[:, ST[2] // 16:16], T.sc[:, ST[2] + 15:256:16], D(0), None, A.add, None, s_2)]
+            o_s = TS(T.off[:, so:so + nk], T.sc[:, 256 + 15:256 + 16 * nk:16], sm, None, A.add, None, s_2)
+            continue
+        seq = T.gt[:, 256:256 + ns]
+        if k == lastsq:
+            v_0, v_1 = W(0), W(1)
         if ns:
-            o_s = TS(T.off[:, so:so + nk], T.sc[:, 256 + 15:256 + 16 * nk:16], sm, None, A.add, None, s_b)
+            x_2 = MM(T.px2[:, 0:ns], T.lx[:], seq, True, True, gg[2])
+        if k == lastsq:
+            v_2 = W(2)
+            w_ev = [WE(0, v_0), WE(1, v_1), WE(2, v_2)]
+        if ns:
+            r_2 = MM(T.pr1[:, 0:ns], T.lr[:], seq, True, True)
+            m_s = ACT(T.m[:, 16 * so:16 * so + ns], T.pr1[:, 0:ns], F.Sign, D(2), r_2)
+            s_2 = SCAN(T.sc[:, 256:256 + ns], T.cs[:, 0:ns], T.px2[:, 0:ns], x_2)
+            o_s = TS(T.off[:, so:so + nk], T.sc[:, 256 + 15:256 + 16 * nk:16], sm, None, A.add, None, s_2)
 
     win = wins[0][:, 256:512] if rank == 0 else wins[last % 2][:, 0:256]
     g_f = TT(T.gt[:, 256:320], win.indirect(T.off[:, 16:20]), T.m[:, 256:320], A.mult, o_s, m_s, *w_ev)
-    f_1 = MM(T.ps[0:64, 0:64], T.gt[:, 256:320], T.ef[:], True, True, g_f)
-    f_2 = TT(T.zf[0:64, :], T.ps[0:64, 0:64], T.zm[0:64, :], A.mult, f_1)
-    MM(T.pt[:, 0:32], T.mu[0:64, 0:128], T.zf[0:64, 0:32], True, False, f_2)
-    f_3 = MM(T.pt[:, 0:32], T.mu[0:64, 0:128], T.zf[0:64, 32:64], False, True)
-    f_4 = TS(T.offy[:], T.pt[:, 0:32], 128.0, None, A.add, None, f_3)
-    ready = [f_4, ("ax", arrive), ("dx", 16)]
-    y_a = CP(T.yo[:, 0:256], T.xw[:].indirect(T.offy[:, 0:16]), *ready)
-    y_b = ACT(T.yo[:, 256:512], T.xw[:].indirect(T.offy[:, 16:32]), F.Identity, -0.0, *ready)
+    f_1 = MM(T.pr1[0:64, 0:64], T.gt[:, 256:320], T.ef[:], True, True, g_f)
+    f_2 = TT(T.zf[0:64, :], T.pr1[0:64, 0:64], T.zm[0:64, :], A.mult, f_1)
+    MM(T.pr2[:, 0:32], T.mu[0:64, 0:128], T.zf[0:64, 0:32], True, False, f_2)
+    f_3 = MM(T.pr2[:, 0:32], T.mu[0:64, 0:128], T.zf[0:64, 32:64], False, True)
+    f_4 = TS(T.offy[:], T.pr2[:, 0:32], 128.0, None, A.add, None, f_3)
+    y_a = CP(T.yo[:, 0:256], T.xw[:].indirect(T.offy[:, 0:16]), f_4, *ready)
+    y_b = ACT(T.yo[:, 256:512], T.xw[:].indirect(T.offy[:, 16:32]), F.Identity, -0.0, f_4, *ready)
     wait("y", [y_a])
     g.sync.dma_start(T.y[:, 0:256], T.yo[:, 0:256]).then_inc(sem.dy, 16)
     wait("s", [y_b])
     g.scalar.dma_start(T.y[:, 256:512], T.yo[:, 256:512]).then_inc(sem.dy, 16)
-    sent = 2 * sum(len(bits(mk[d])) for d in others)
-    wait("i", [("rl", sent), ("sv", cnt["sv"]), ("ss", cnt["ss"]), ("sp", cnt["sp"]), ("dy", 32)])
+    wait("i", [("rl", sent[0]), ("sv", cnt["sv"]), ("ss", cnt["ss"]), ("sp", cnt["sp"]), ("dy", 32)])
     wait("v", [("si", cnt["si"])])

@@ -6,32 +6,38 @@ SCRATCH = {
     "nxs": ("sbuf", [128, 64], "int32"),
     "xw": ("sbuf", [128, 2048], BF),
     "yo": ("sbuf", [128, 512], BF),
-    "pi": ("sbuf", [128, 1], "int32"), "v16": ("sbuf", [128, 16], "int32"),
+    "pi": ("sbuf", [128, 1], "int32"), "vr": ("sbuf", [128, 16], FL),
     "ju": ("sbuf", [128, 128], BF), "jg": ("sbuf", [128, 128], BF), "jq": ("sbuf", [128, 128], BF),
-    "jj": ("sbuf", [128, 256], BF), "jv": ("sbuf", [128, 64], BF), "je": ("sbuf", [128, 64], BF),
-    "pc": ("sbuf", [128, 16], "int32"), "pf": ("sbuf", [128, 16], FL), "pd": ("sbuf", [128, 32], FL),
-    "l16": ("sbuf", [128, 2], "uint16"), "lz": ("sbuf", [128, 16], "uint16"),
+    "jp": ("sbuf", [128, 128], BF), "jw": ("sbuf", [128, 64], BF), "jj": ("sbuf", [128, 256], BF),
+    "pc": ("sbuf", [128, 16], "int32"), "pf": ("sbuf", [128, 8], FL), "pd": ("sbuf", [128, 40], FL),
+    "kb": ("sbuf", [128, 8], FL), "zo": ("sbuf", [128, 80], BF),
+    "l16": ("sbuf", [128, 2], "uint16"), "lz": ("sbuf", [128, 4], "uint16"),
     "i0": ("sbuf", [128, 16], FL), "q3b": ("sbuf", [128, 16], FL),
-    "mu": ("sbuf", [128, 256], BF), "cs": ("sbuf", [128, 256], BF),
+    "mu": ("sbuf", [128, 128], BF), "mw": ("sbuf", [128, 64], BF), "cs": ("sbuf", [128, 128], BF),
     "bd": ("sbuf", [128, 128], BF), "lx": ("sbuf", [128, 128], BF), "lr": ("sbuf", [128, 128], BF),
-    "ca": ("sbuf", [128, 128], BF), "cb": ("sbuf", [128, 128], BF), "cc": ("sbuf", [128, 128], BF),
-    "cd": ("sbuf", [128, 128], BF), "ce": ("sbuf", [128, 128], BF), "cf": ("sbuf", [128, 128], BF),
+    "eye": ("sbuf", [128, 768], BF),
+    "bdv": ("sbuf", [128, 512], BF), "ltv": ("sbuf", [128, 512], BF), "lhv": ("sbuf", [128, 512], BF),
+    "ck": ("sbuf", [128, 768], BF),
     "lw": ("sbuf", [128, 128], BF), "lwt": ("sbuf", [128, 128], BF), "lwh": ("sbuf", [128, 128], BF),
-    "on1": ("sbuf", [128, 128], BF), "on2": ("sbuf", [128, 128], BF),
-    "ef": ("sbuf", [128, 64], BF), "zm": ("sbuf", [128, 64], BF),
+    "on": ("sbuf", [128, 256], BF),
+    "ef": ("sbuf", [128, 16], BF),
     "t0": ("sbuf", [128, 16], "int32"), "h0": ("sbuf", [128, 16], "int32"),
     "e0": ("sbuf", [128, 16], FL), "e1": ("sbuf", [128, 16], BF), "e2": ("sbuf", [128, 16], BF),
     "er": ("sbuf", [128, 16], FL), "hd": ("sbuf", [128, 4], "int32"), "hf": ("sbuf", [128, 1], FL),
-    "zt": ("sbuf", [128, 256], BF), "zh": ("sbuf", [128, 256], BF),
+    "zt": ("sbuf", [128, 64], BF), "zh": ("sbuf", [128, 64], BF),
     "w0": ("sbuf", [128, 512], BF), "w1": ("sbuf", [128, 512], BF),
     "m": ("sbuf", [128, 320], BF), "gt": ("sbuf", [128, 320], BF), "sc": ("sbuf", [128, 320], FL),
     "off": ("sbuf", [128, 20], "uint16"), "zf": ("sbuf", [128, 64], BF), "offy": ("sbuf", [128, 32], "uint16"),
-    "px0": ("psum", [128, 512], FL), "px1": ("psum", [128, 512], FL), "px2": ("psum", [128, 512], FL),
-    "pw0": ("psum", [128, 512], FL), "pw1": ("psum", [128, 512], FL), "pw2": ("psum", [128, 512], FL),
-    "pr1": ("psum", [128, 512], FL), "pr2": ("psum", [128, 512], FL),
 }
+for _k in range(8):
+    SCRATCH["b%d" % _k] = ("psum", [128, 512], FL)
 SEMAPHORES = ["sv", "ss", "sp", "si", "dn", "dx", "dy", "rl", "an", "ax", "ap"]
-SZ = [64, 128, 64]
+
+SZ, ST = [96, 96, 64], [0, 96, 192]
+BX, BW, BR, RO = [0, 1, 2], [3, 6, 7], [3, 4, 5], [96, 0, 0]
+ORD = {"v": "g0 o2- oS- g1 g2 c0 c1 o0 e2 o1 c2".split(),
+       "s": "m0 e0 e1 m1 m2 mS".split(),
+       "p": "x0 r0 w0 x1 w1 w2 x2 r1 r2".split()}
 
 
 def bits(m):
@@ -67,6 +73,8 @@ def rank_program(g, core, T, topo):
     def wait(q, deps):
         need = {}
         for d in deps:
+            if isinstance(d, dict):
+                d = d["tok"]
             need[d[0]] = max(need.get(d[0], 0), d[1])
         for s in sorted(need):
             if seen.get((q, s), 0) < need[s]:
@@ -79,31 +87,53 @@ def rank_program(g, core, T, topo):
         cnt[S[q]] = cnt.get(S[q], 0) + 1
         return (S[q], cnt[S[q]])
 
-    def V(call, *deps):
-        return op("v", call, deps)
+    lists = {"v": [], "s": [], "p": []}
 
-    def TS(out, in0, s1, s2, o1, o2, *deps):
+    def N(q, calls, *deps):
+        return {"q": q, "calls": calls if isinstance(calls, list) else [calls], "deps": [d for d in deps if d], "tok": None}
+
+    def put(*nodes):
+        for n in nodes:
+            lists[n["q"]].append(n)
+        return nodes[-1] if nodes else None
+
+    def flush():
+        moved = True
+        while moved:
+            moved = False
+            for q in "vps":
+                while lists[q] and not any(isinstance(d, dict) and d["tok"] is None for d in lists[q][0]["deps"]):
+                    n = lists[q].pop(0)
+                    for j, c in enumerate(n["calls"]):
+                        n["tok"] = op(q, c, n["deps"] if j == 0 else ())
+                    moved = True
+        assert not any(lists.values())
+
+    def mm(out, l, r, a=True, z=True):
+        return lambda e: e.matmul(out, l, r, a, z)
+
+    def act(out, in_, f, b=0.0, m=1.0):
+        return lambda e: e.activation(out, in_, f, bias=b, scale=m)
+
+    def ts(out, in0, s1, o1, s2=None, o2=None):
         if o2 is None:
-            return V(lambda e: e.tensor_scalar(out, in0, s1, None, o1), *deps)
-        return V(lambda e: e.tensor_scalar(out, in0, s1, s2, o1, o2), *deps)
+            return lambda e: e.tensor_scalar(out, in0, s1, None, o1)
+        return lambda e: e.tensor_scalar(out, in0, s1, s2, o1, o2)
 
-    def TT(out, a, b, o, *deps):
-        return V(lambda e: e.tensor_tensor(out, a, b, o), *deps)
+    def tt(out, a, b, o):
+        return lambda e: e.tensor_tensor(out, a, b, o)
 
-    def CP(out, a, *deps):
-        return V(lambda e: e.tensor_copy(out, a), *deps)
+    def cp(out, a):
+        return lambda e: e.tensor_copy(out, a)
 
-    def SCAN(out, c, x, *deps):
-        return V(lambda e: e.tensor_tensor_scan(out, c, x, 0.0, A.add, A.max), *deps)
+    def scan(out, c, x):
+        return lambda e: e.tensor_tensor_scan(out, c, x, 0.0, A.add, A.max)
 
-    def MM(out, l, r, a, z, *deps):
-        return op("p", lambda e: e.matmul(out, l, r, a, z), deps)
-
-    def ACT(out, a, f, b, *deps):
-        return op("s", lambda e: e.activation(out, a, f, bias=b), deps)
+    def TS(out, in0, s1, o1, s2=None, o2=None, deps=()):
+        return op("v", ts(out, in0, s1, o1, s2, o2), deps)
 
     def LIN(out, a, m, b, *deps):
-        return op("s", lambda e: e.activation(out, a, F.Identity, bias=b, scale=m), deps)
+        return op("s", act(out, a, F.Identity, b, m), deps)
 
     c0 = 16 * rank
     slot = T.nxs[:, c0:c0 + 16]
@@ -113,17 +143,18 @@ def rank_program(g, core, T, topo):
     g.sync.dma_start(T.xw[:, 512 * rank:512 * rank + 512], T.x[:, :]).then_inc(sem.dx, 16)
     ms = []
     for a, b in {0: [(32, 64), (64, 128)], 1: [(0, 32), (64, 128)], 2: [(0, 64), (96, 128)], 3: [(0, 64), (64, 96)]}[rank]:
-        ms.append(V(lambda e: e.memset(T.nxs[a:b, c0:c0 + 16], 0)))
+        ms.append(op("v", lambda e: e.memset(T.nxs[a:b, c0:c0 + 16], 0)))
 
     def IO(out, pat, base=0, cm=0, flag=True):
         if flag:
             return op("i", lambda e: e.iota(out, pat, base, cm, allow_small_or_imprecise_dtypes=True))
         return op("i", lambda e: e.iota(out, pat, base, cm))
     i_p = IO(T.pi[:], [[0, 1]], 0, 1, False)
-    i_v = IO(T.v16[:], [[1, 16]], 0, 0, False)
-    i_u = IO(T.ju[:], [[0, 8], [1, 16]])
+    i_r = IO(T.vr[:], [[1, 16]])
+    i_w = IO(T.jw[:], [[0, 16], [1, 4]])
     i_g = IO(T.jg[:], [[1, 8], [0, 16]])
     i_q = IO(T.jq[:], [[0, 8], [1, 8], [8, 2]])
+
     sent = [0]
 
     def send(dests, ap):
@@ -142,11 +173,11 @@ def rank_program(g, core, T, topo):
         return T.xw[:, 512 * r_:512 * r_ + 512]
     wait("i", [("dn", 32)] + ms)
     send([(d, sem.an) for d in others], slot)
+    i_u = IO(T.ju[:], [[0, 8], [1, 16]])
+    i_y = IO(T.jp[:], [[1, 128]])
     i_j = IO(T.jj[:], [[1, 256]], -128)
     wait("i", [("dx", 16)])
     send([(near, sem.ax), (peer, sem.ap)], xs(core))
-    i_7 = IO(T.jv[:], [[0, 8], [1, 8]])
-    i_e = IO(T.je[:], [[0, 2], [1, 4], [0, 8]])
     nearpeer = [d for d in others if d not in (near, peer)][0]
     n_an = sum(part(d, [e for e in T.cores if e != d], core) for d in others)
     n_ap = part(peer, [nearpeer, core], core)
@@ -155,21 +186,26 @@ def rank_program(g, core, T, topo):
     wait("i", [("ap", n_ap)])
     send([(near, sem.ax)], xs(peer))
 
-    pc, pf, pd = T.pc, T.pf, T.pd
-    for k, ops in enumerate([(0, 15), (4, 15), (1, 7), (0, 1), (0, 240), (1, 112)]):
-        c_ = TS(pc[:, k:k + 1], T.pi[:], ops[0], ops[1], A.logical_shift_right, A.bitwise_and, i_p)
-    c_f = CP(pf[:, 0:6], pc[:, 0:6], c_)
-    u, gc, q3, ch = pf[:, 0:1], pf[:, 1:2], pf[:, 2:3], pf[:, 3:4]
+    pc, pf, pd, kb = T.pc, T.pf, T.pd, T.kb
+    SR, AND, EQ = A.logical_shift_right, A.bitwise_and, A.is_equal
 
     def D(k):
         return pd[:, k:k + 1]
-    CP(T.lz[:], T.v16[:], i_v)
-    c_7 = TS(D(7), gc, 7.0, None, A.is_equal, None, c_f)
-    TS(T.l16[:, 0:1], pf[:, 5:6], u, None, A.add, None)
-    c_b = TS(D(6), D(7), -8.0, gc, A.mult, A.add, c_7)
-    TS(T.mu[:, 0:128], T.ju[:], u, None, A.is_equal, None, i_u)
-    c_b = TS(D(18), D(6), 1.0, None, A.add, None, c_b)
-    c_u = TS(T.mu[:, 128:256], T.ju[:], u, None, A.is_equal, None)
+
+    def of(t, v):
+        return t[:, 128 * v:128 * v + 128]
+    ca, cb, cc, cd, ce, cf = [of(T.ck, v) for v in range(6)]
+    for k, (a, b) in enumerate([(0, 15), (4, 15), (1, 7), (0, 1), (0, 240), (1, 112), (2, 3), (0, 3)]):
+        c_ = TS(pc[:, k:k + 1], T.pi[:], a, SR, b, AND, [i_p])
+    c_f = op("v", cp(pf[:, 0:8], pc[:, 0:8]), [c_])
+    u, gc, q3, ch, uw, uv = pf[:, 0:1], pf[:, 1:2], pf[:, 2:3], pf[:, 3:4], pf[:, 6:7], pf[:, 7:8]
+    c_7 = TS(D(7), gc, 7.0, EQ, deps=[c_f])
+    TS(T.l16[:, 0:1], pf[:, 5:6], u, A.add)
+    TS(T.lz[:], T.vr[:, 0:4], 4.0, A.mult, uw, A.add, [i_r])
+    c_b = TS(D(6), D(7), -8.0, A.mult, gc, A.add, [c_7])
+    c_v = TS(pd[:, 24:28], T.vr[:, 0:4], uv, EQ)
+    TS(T.mw[:], T.jw[:], uw, EQ, deps=[i_w])
+    c_b = TS(D(18), D(6), 1.0, A.add, deps=[c_b])
     k_8 = LIN(D(8), D(7), 1.0, -0.5, c_7)
     k_e = LIN(D(14), gc, 1.0, 8.0)
     k_f = LIN(D(15), D(18), 1.0, 8.0, c_b)
@@ -179,74 +215,78 @@ def rank_program(g, core, T, topo):
     LIN(D(2), q3, -1.0, 0.5)
     k_b = LIN(D(11), q3, -256.0, 2096128.5)
     k_a = LIN(D(10), pf[:, 4:5], 16.0, u)
-    LIN(D(0), u, 256.0, -3712.0)
-    k_1 = LIN(D(1), u, 256.0, -3456.0)
-    LIN(T.i0[:], T.ju[:, 0:16], 16.0, D(10), i_u, k_a)
-    k_q = LIN(T.q3b[:], T.ju[:, 0:16], 0.0, D(11), k_b)
-    LIN(T.cs[:], T.mu[:], -16640.0, 256.0, c_u)
-    TS(T.bd[:], T.jg[:], gc, None, A.is_equal, None, i_g)
-    TS(T.cc[:], T.jq[:], gc, 0.5, A.is_equal, A.mult, i_q)
-    TS(T.ca[:], T.jq[:], D(14), 0.5, A.is_equal, A.mult, k_e)
-    c_2 = TS(T.cd[:], T.jq[:], D(18), D(8), A.is_equal, A.mult, k_8, c_b)
-    c_1 = TS(T.cb[:], T.jq[:], D(15), D(8), A.is_equal, A.mult, k_f)
-    TT(T.lwt[:], T.cc[:], T.cd[:], A.add, c_2)
-    TT(T.lwh[:], T.ca[:], T.cb[:], A.add, c_1)
-    TS(D(4), u, 0.0, -128.0, A.is_equal, A.mult)
-    V(lambda e: e.memset(T.on1[:], -1.0))
-    V(lambda e: e.memset(T.on2[:], -256.0))
-    TS(T.ce[:], T.jq[:], D(13), 0.5, A.is_equal, A.mult, k_d)
-    c_3 = TS(T.cf[:], T.jq[:], D(16), D(8), A.is_equal, A.mult, k_g)
-    TS(T.lx[:], T.jg[:], gc, D(5), A.is_equal, A.mult, k_5)
-    TT(T.lw[:], T.ce[:], T.cf[:], A.add, c_3)
-    TS(T.lr[:], T.jg[:], gc, ch, A.is_equal, A.mult)
-    c_9 = TS(D(9), u, 1.0, 3.0, A.is_equal, A.mult)
-    c_3 = TS(D(3), u, 0.0, None, A.is_equal, None)
-    k_h = LIN(D(17), ch, 0.5, D(9), c_9)
-    idw = [LIN(w[:, 256:512], T.jj[:], D(3), D(17), i_j, k_h, c_3) for w in (T.w0, T.w1)]
+    LIN(D(0), u, 512.0, -7552.0)
+    k_6 = LIN(D(19), ch, 256.0, 0.0)
+    c_d = TS(T.bd[:], T.jg[:], gc, EQ, deps=[i_g])
+    TS(cc, T.jq[:], gc, EQ, 0.5, A.mult, [i_q])
+    TS(ca, T.jq[:], D(14), EQ, 0.5, A.mult, [k_e])
+    c_2 = TS(cd, T.jq[:], D(18), EQ, D(8), A.mult, [k_8, c_b])
+    c_1 = TS(cb, T.jq[:], D(15), EQ, D(8), A.mult, [k_f])
+    c_h = op("v", tt(T.lwh[:], ca, cb, A.add), [c_1])
+    c_t = op("v", tt(T.lwt[:], cc, cd, A.add))
+    k_i = LIN(T.i0[:], T.vr[:], 16.0, D(10), i_r, k_a)
+    LIN(T.q3b[:], T.vr[:], 0.0, D(11), k_b)
+    for dst, src, dep in ((T.bdv, T.bd, c_d), (T.lhv, T.lwh, c_h), (T.ltv, T.lwt, c_t)):
+        for v in range(4):
+            k_l = LIN(of(dst, v), src[:], D(24 + v), 0.0, c_v, dep)
+    op("v", lambda e: e.memset(of(T.on, 0), -1.0))
+    op("v", lambda e: e.memset(of(T.on, 1), -256.0))
+    TS(D(4), u, 0.0, EQ, -128.0, A.mult)
+    TS(ce, T.jq[:], D(13), EQ, 0.5, A.mult, [k_d])
+    c_3 = TS(cf, T.jq[:], D(16), EQ, D(8), A.mult, [k_g])
+    TS(T.lx[:], T.jg[:], gc, EQ, D(5), A.mult, [k_5])
+    TS(T.lr[:], T.jg[:], gc, EQ, ch, A.mult)
+    op("v", tt(T.lw[:], ce, cf, A.add), [c_3])
     for k in range(7):
-        c_ = TS(pc[:, 6 + k:7 + k], T.pi[:], k, 1, A.logical_shift_right, A.bitwise_and)
-    c_f = CP(pf[:, 6:13], pc[:, 6:13], c_)
-    TS(D(19), pf[:, 6:7], -256.0, 256.0, A.mult, A.add, c_f)
-    TS(pd[:, 20:27], pf[:, 6:13], -256.0, D(1), A.mult, A.add, k_1)
-    extra = [lambda: TS(T.ef[:, 0:32], T.jv[:, 0:32], gc, D(5), A.is_equal, A.mult, i_7),
-             lambda: TS(T.ef[:, 32:64], T.jv[:, 32:64], gc, ch, A.is_equal, A.mult),
-             lambda: TS(T.zm[:, 0:32], T.je[:, 0:32], gc, None, A.is_equal, None, i_e),
-             lambda: TS(T.zm[:, 32:64], T.je[:, 32:64], gc, 256.0, A.is_equal, A.mult)]
+        c_ = TS(pc[:, 8 + k:9 + k], T.pi[:], k, SR, 1, AND)
+    op("v", cp(D(28), T.pi[:]))
+    op("v", lambda e: e.memset(T.zo[:, 0:64], 0.0))
+    op("v", lambda e: e.memset(T.zo[:, 64:80], 1.0))
+    n_k = TS(kb[:, 0:7], pc[:, 8:15], -256.0, A.mult, 256.0, A.add, [c_])
+    c_u = TS(T.mu[:], T.ju[:], u, EQ, deps=[i_u])
+    k_s = LIN(T.cs[:], T.mu[:], -33280.0, 512.0, c_u)
+    c_9 = TS(D(9), u, 1.0, EQ, 3.0, A.mult)
+    c_3 = TS(D(3), u, 0.0, EQ)
+    k_h = LIN(D(17), ch, 0.5, D(9), c_9)
+    idw = [LIN(T.w0[:, 256:512], T.jj[:], D(3), D(17), i_j, k_h, c_3)]
+    late = [N("v", ts(of(T.eye, k), T.jp[:], D(28), EQ, kb[:, k + 1:k + 2], A.mult), i_y, n_k) for k in range(6)]
+    late.append(N("v", ts(T.ef[:, 0:16:2], T.jg[:, 0:128:16], gc, EQ, D(5), A.mult), k_5))
+    n_e = N("v", ts(T.ef[:, 1:16:2], T.jg[:, 0:128:16], gc, EQ, D(19), A.mult), k_6)
+    late.append(n_e)
 
-    wait("v", [("dn", 32), ("an", n_an), ("sv", cnt["sv"]), k_q])
+    B = [T["b%d" % k] for k in range(8)]
+    wait("v", [("dn", 32), ("an", n_an), ("sv", cnt["sv"])])
     nx = T.nxs[:].indirect(T.l16[:, 0:1])
-    a_h = TS(T.h0[:], nx, 8, None, A.logical_shift_right, None)
-    a_t = TS(T.t0[:], nx, 255, None, A.bitwise_and, None)
-    h_1 = TT(T.e0[:], nx, T.i0[:], A.not_equal)
-    z_h = TT(T.zh[:], T.h0[:].indirect(T.lz[:]), T.mu[:], A.mult, a_h)
-    TT(T.e1[:], T.e0[:], T.t0[:], A.mult, a_t, h_1)
-    h_2 = TT(T.e2[:], T.e0[:], T.h0[:], A.mult)
-    z_a = TT(T.zt[:, 0:192], T.t0[:].indirect(T.lz[:, 0:12]), T.mu[:, 0:192], A.mult)
-    z_b = TT(T.zt[:, 192:256], T.t0[:].indirect(T.lz[:, 12:16]), T.mu[:, 192:256], A.mult)
-    o_t = CP(T.off[:, 0:16], T.t0[:])
-    MM(T.pw0[:, 0:192], T.lwh[:], T.zh[:, 0:192], True, False, z_h)
-    MM(T.pr2[:, 0:16], T.on1[:], T.e1[:], True, False, h_2)
-    h_5 = MM(T.pr2[:, 0:16], T.on2[:], T.e2[:], False, True)
-    MM(T.pw1[:, 0:64], T.lwh[:], T.zh[:, 192:256], True, False)
-    r_a = MM(T.px0[:, 0:64], T.bd[:], T.zh[:, 0:64], True, True)
-    w_0 = MM(T.pw0[:, 0:192], T.lwt[:], T.zt[:, 0:192], False, True, z_a)
-    w_1 = MM(T.pw1[:, 0:64], T.lwt[:], T.zt[:, 192:256], False, True, z_b)
-    r_b = MM(T.pr1[:, 0:192], T.bd[:], T.zh[:, 64:256], True, True)
-    h_6 = op("s", lambda e: e.activation(T.er[:], T.pr2[:, 0:16], F.Copy, accum_out=T.hf[:]), [h_5])
-    m_a = ACT(T.m[:, 0:64], T.px0[:, 0:64], F.Sign, D(2), r_a)
-    m_s = ACT(T.m[:, 256:272], T.q3b[:], F.Sign, T.hf[:], h_6)
-    w_ev = [ACT(T.w0[:, 0:192], T.pw0[:, 0:192], F.Identity, D(4), w_0)]
-    m_b = ACT(T.m[:, 64:256], T.pr1[:, 0:192], F.Sign, D(2), r_b)
-    h_7 = TS(T.hd[:, 0:1], T.hf[:], 2096128.0, None, A.add, None, h_6)
-    w_ev.append(TS(T.w0[:, 192:256], T.pw1[:, 0:64], D(4), None, A.add, None, w_1))
-    h_8 = TS(T.hd[:, 1:2], T.hd[:, 0:1], 255, None, A.bitwise_and, None, h_7)
-    o_s = TS(T.off[:, 16:17], T.hd[:, 1:2], D(19), None, A.add, None, h_8)
+    h_0 = put(N("v", ts(T.h0[:], nx, 8, SR)))
+    t_0 = put(N("v", ts(T.t0[:], nx, 255, AND)))
+    e_0 = put(N("v", tt(T.e0[:], nx, T.i0[:], A.not_equal), k_i))
+    z_h = put(N("v", tt(T.zh[:], T.h0[:].indirect(T.lz[:]), T.mw[:], A.mult), h_0))
+    put(N("v", tt(T.e1[:], T.e0[:], T.t0[:], A.mult), e_0))
+    e_2 = put(N("v", tt(T.e2[:], T.e0[:], T.h0[:], A.mult)))
+    z_t = put(N("v", tt(T.zt[:], T.t0[:].indirect(T.lz[:]), T.mw[:], A.mult), t_0))
+    o_t = put(N("v", cp(T.off[:, 0:16], T.t0[:])))
+    for v in range(4):
+        put(N("p", mm(B[v][:, 0:64], of(T.lhv, v), T.zh[:], True, False), z_h, k_l))
+    h_5 = put(N("p", [mm(B[5][:, 0:16], of(T.on, 0), T.e1[:], True, False), mm(B[5][:, 0:16], of(T.on, 1), T.e2[:], False, True)], e_2))
+    R = [put(N("p", mm(B[4][:, v:256:4], of(T.bdv, v), T.zh[:]))) for v in range(4)]
+    W = [put(N("p", mm(B[v][:, 0:64], of(T.ltv, v), T.zt[:], False, True), z_t)) for v in range(4)]
+    h_6 = N("s", lambda e: e.activation(T.er[:], B[5][:, 0:16], F.Copy, accum_out=T.hf[:]), h_5)
+    m_a = N("s", act(T.m[:, 0:96], B[4][:, 0:96], F.Sign, D(2)), R[3])
+    m_b = N("s", act(T.m[:, 96:256], B[4][:, 96:256], F.Sign, D(2)), R[3])
+    m_s = N("s", act(T.m[:, 256:272], T.q3b[:], F.Sign, T.hf[:]), h_6)
+    w_ev = [N("v", ts(T.w0[:, v:256:4], B[v][:, 0:64], D(4), A.add), W[v]) if v % 2 == 0 else
+            N("s", act(T.w0[:, v:256:4], B[v][:, 0:64], F.Identity, D(4)), W[v]) for v in range(4)]
+    idw.append(N("s", act(T.w1[:, 256:512], T.jj[:], F.Identity, D(17), D(3))))
+    put(h_6, m_a, w_ev[1], w_ev[3], m_b, m_s, idw[1])
+    h_7 = N("v", ts(T.hd[:, 0:1], T.hf[:], 2096128.0, A.add), h_6)
+    h_8 = N("v", ts(T.hd[:, 1:2], T.hd[:, 0:1], 255, AND), h_7)
+    o_s = N("v", ts(T.off[:, 16:17], T.hd[:, 1:2], kb[:, 0:1], A.add), h_8, n_k)
+    put(*late[:6])
+    put(h_7, w_ev[0], w_ev[2], h_8)
+    put(*late[6:])
 
     wins = [T.w0, T.w1]
-    px, pw, pr = [T.px0, T.px1, T.px2], [T.pw0, T.pw1, T.pw2], [T.pw0, T.pr1, T.pr2]
-    ST = [0, SZ[0], SZ[0] + SZ[1]]
-    RO = [SZ[0], 0, 0]
-    m_p, o_p = [m_a, m_b, m_b], [o_t, o_t, o_t]
+    m_p, o_p, prev = [m_a, m_b, m_b], [o_t, o_t, o_t], {"oS": o_s}
     last = {0: 9, 1: 9, 2: 10, 3: 10}[rank]
     lastsq = 7 if rank == 0 else last - 1
     for k in range(last):
@@ -255,79 +295,70 @@ def rank_program(g, core, T, topo):
         ns = {7: 16, 8: 32, 9: 64 if rank == 3 else 0}.get(k, 16)
         so = {7: 17, 8: 18}.get(k, 16)
         nk = ns // 16
-        wd = [SZ[0], SZ[1], SZ[2] + ns]
-        sm = D(20 + k + 1) if k + 1 <= 6 else D(0)
-        gg = []
+        nd, wd = {}, [SZ[0], SZ[1], SZ[2] + (ns if square else 0)]
         if k <= lastsq:
             for i in range(3):
                 a, b = ST[i], ST[i] + wd[i]
-                dep = [o_p[i], m_p[i]] + w_ev + ([o_s, m_s] + idw if i == 2 else [])
-                gg.append(TT(T.gt[:, a:b], cur[:].indirect(T.off[:, a // 16:b // 16]), T.m[:, a:b], A.mult, *dep))
-        else:
-            gg = [None, None, TT(T.gt[:, 256:256 + ns], cur[:].indirect(T.off[:, 16:16 + nk]), T.m[:, 256:256 + ns],
-                                 A.mult, o_s, m_s, *w_ev)]
-
-        def X(i):
-            return MM(px[i][:, 0:wd[i]], T.lx[:], T.gt[:, ST[i]:ST[i] + wd[i]], True, True, gg[i])
-
-        def R(i):
-            return MM(pr[i][:, RO[i]:RO[i] + wd[i]], T.lr[:], T.gt[:, ST[i]:ST[i] + wd[i]], True, True, gg[i])
-
-        def W(i):
-            return MM(pw[i][:, 0:SZ[i]], T.lw[:], T.gt[:, ST[i]:ST[i] + SZ[i]], True, True, gg[i])
-
-        def WE(i, dep):
-            return ACT(nxt[:, ST[i]:ST[i] + SZ[i]], pw[i][:, 0:SZ[i]], F.Copy, 0.0, dep)
-
-        def ME(i, n, dep):
-            return ACT(T.m[:, ST[i]:ST[i] + n], pr[i][:, RO[i]:RO[i] + n], F.Sign, D(2), dep)
-
-        def SC(i, dep):
-            return SCAN(T.sc[:, ST[i]:ST[i] + wd[i]], T.cs[:, 0:wd[i]], px[i][:, 0:wd[i]], dep)
+                seq = [o_s, m_s] + idw if i == 2 and square else []
+                nd["g%d" % i] = N("v", tt(T.gt[:, a:b], cur[:].indirect(T.off[:, a // 16:b // 16]), T.m[:, a:b], A.mult),
+                                  o_p[i], m_p[i], *(w_ev + seq))
+                nd["w%d" % i] = N("p", mm(B[BW[i]][:, 0:SZ[i]], T.lw[:], T.gt[:, a:a + SZ[i]]), nd["g%d" % i])
         if square:
-            x_0, _, v_0 = X(0), R(0), W(0)
-            x_1, v_1 = X(1), W(1)
-            x_2, v_2 = X(2), W(2)
-            r_1, r_2 = R(1), R(2)
-            m_0 = ME(0, SZ[0], v_0)
-            w_ev = [WE(0, v_0), WE(1, v_1), WE(2, v_2)]
-            m_p = [m_0, ME(1, SZ[1], r_1), ME(2, wd[2] if so == 16 else SZ[2], r_2)]
-            if so == 16:
-                m_s = m_p[2]
-            else:
-                m_s = ACT(T.m[:, 16 * so:16 * so + ns], T.pr2[:, SZ[2]:wd[2]], F.Sign, D(2), r_2)
-            SC(0, x_0)
-            if 2 <= k < 6:
-                extra[k - 2]()
-            s_1 = SC(1, x_1)
-            s_2 = SC(2, x_2)
-            o_1 = TS(T.off[:, 0:ST[2] // 16], T.sc[:, 15:ST[2]:16], D(0), None, A.add, None, s_1)
-            o_p = [o_1, o_1, TS(T.off[:, ST[2] // 16:16], T.sc[:, ST[2] + 15:256:16], D(0), None, A.add, None, s_2)]
-            o_s = TS(T.off[:, so:so + nk], T.sc[:, 256 + 15:256 + 16 * nk:16], sm, None, A.add, None, s_2)
+            for i in range(3):
+                a, n, gi, wi = ST[i], wd[i], nd["g%d" % i], nd["w%d" % i]
+                ab, px, pr, pw = T.gt[:, a:a + n], B[BX[i]][:, 0:n], B[BR[i]], B[BW[i]]
+                add = i == 2 and k < 6
+                x_ = [mm(px, T.lx[:], ab, True, not add)] + ([mm(px, of(T.eye, k), T.zo[:], False, True)] if add else [])
+                nd["x%d" % i] = N("p", x_, gi)
+                ri = nd["r%d" % i] = N("p", mm(pr[:, RO[i]:RO[i] + n], T.lr[:], ab), gi)
+                both = [ri, wi] if BR[i] == BW[i] else []
+                n1 = n if so == 16 else SZ[i]
+                m_p[i] = nd["m%d" % i] = N("s", act(T.m[:, a:a + n1], pr[:, RO[i]:RO[i] + n1], F.Sign, D(2)), ri, *both)
+                out, in_ = nxt[:, a:a + SZ[i]], pw[:, 0:SZ[i]]
+                nd["e%d" % i] = N("v", cp(out, in_), wi) if i == 2 else N("s", act(out, in_, F.Copy), wi, *both)
+                ci = nd["c%d" % i] = N("v", scan(T.sc[:, a:a + n], T.cs[:, 0:n], px), nd["x%d" % i], k_s)
+                o_p[i] = nd["o%d" % i] = N("v", ts(T.off[:, a // 16:(a + n1) // 16], T.sc[:, a + 15:a + n1:16], D(0), A.add), ci)
+            m_s, o_s = m_p[2], o_p[2]
+            if so != 16:
+                m_s = nd["mS"] = N("s", act(T.m[:, 16 * so:16 * so + ns], B[BR[2]][:, 64:64 + ns], F.Sign, D(2)), ri)
+                o_s = nd["oS"] = N("v", ts(T.off[:, so:so + nk], T.sc[:, 256 + 15:256 + ns:16], D(0), A.add), ci)
+            w_ev = [nd["e%d" % i] for i in range(3)]
+            for q in "vps":
+                for nm in ORD[q]:
+                    n = prev.get(nm[:-1]) if nm[-1] == "-" else nd.get(nm)
+                    if n and n["q"] == q:
+                        put(n)
+            prev = nd
             continue
-        seq = T.gt[:, 256:256 + ns]
+        tail = [prev[nm] for nm in ("oS", "o2") if nm in prev]
+        prev = {}
         if k == lastsq:
-            v_0, v_1 = W(0), W(1)
+            put(nd["g0"], nd["w0"])
+            put(*tail)
+            put(nd["g1"], nd["w1"])
         if ns:
-            x_2 = MM(T.px2[:, 0:ns], T.lx[:], seq, True, True, gg[2])
+            ab = T.gt[:, 256:256 + ns]
+            gs = put(N("v", tt(ab, cur[:].indirect(T.off[:, 16:16 + nk]), T.m[:, 256:256 + ns], A.mult), o_s, m_s, *w_ev))
+            x_ = put(N("p", mm(B[2][:, 0:ns], T.lx[:], ab), gs))
+            r_ = put(N("p", mm(B[5][:, 0:ns], T.lr[:], ab)))
         if k == lastsq:
-            v_2 = W(2)
-            w_ev = [WE(0, v_0), WE(1, v_1), WE(2, v_2)]
+            put(nd["g2"], nd["w2"])
+            w_ev = [put(N("s", act(nxt[:, ST[i]:ST[i] + SZ[i]], B[BW[i]][:, 0:SZ[i]], F.Copy), nd["w%d" % i])) for i in range(3)]
         if ns:
-            r_2 = MM(T.pr1[:, 0:ns], T.lr[:], seq, True, True)
-            m_s = ACT(T.m[:, 16 * so:16 * so + ns], T.pr1[:, 0:ns], F.Sign, D(2), r_2)
-            s_2 = SCAN(T.sc[:, 256:256 + ns], T.cs[:, 0:ns], T.px2[:, 0:ns], x_2)
-            o_s = TS(T.off[:, so:so + nk], T.sc[:, 256 + 15:256 + 16 * nk:16], sm, None, A.add, None, s_2)
+            m_s = put(N("s", act(T.m[:, 16 * so:16 * so + ns], B[5][:, 0:ns], F.Sign, D(2)), r_))
+            c_ = put(N("v", scan(T.sc[:, 256:256 + ns], T.cs[:, 0:ns], B[2][:, 0:ns]), x_))
+            o_s = put(N("v", ts(T.off[:, so:so + nk], T.sc[:, 256 + 15:256 + ns:16], D(0), A.add), c_))
 
     win = wins[0][:, 256:512] if rank == 0 else wins[last % 2][:, 0:256]
-    g_f = TT(T.gt[:, 256:320], win.indirect(T.off[:, 16:20]), T.m[:, 256:320], A.mult, o_s, m_s, *w_ev)
-    f_1 = MM(T.pr1[0:64, 0:64], T.gt[:, 256:320], T.ef[:], True, True, g_f)
-    f_2 = TT(T.zf[0:64, :], T.pr1[0:64, 0:64], T.zm[0:64, :], A.mult, f_1)
-    MM(T.pr2[:, 0:32], T.mu[0:64, 0:128], T.zf[0:64, 0:32], True, False, f_2)
-    f_3 = MM(T.pr2[:, 0:32], T.mu[0:64, 0:128], T.zf[0:64, 32:64], False, True)
-    f_4 = TS(T.offy[:], T.pr2[:, 0:32], 128.0, None, A.add, None, f_3)
-    y_a = CP(T.yo[:, 0:256], T.xw[:].indirect(T.offy[:, 0:16]), f_4, *ready)
-    y_b = ACT(T.yo[:, 256:512], T.xw[:].indirect(T.offy[:, 16:32]), F.Identity, -0.0, f_4, *ready)
+    g_f = put(N("v", tt(T.gt[:, 256:320], win.indirect(T.off[:, 16:20]), T.m[:, 256:320], A.mult), o_s, m_s, *(w_ev + idw)))
+    f_1 = put(N("p", [mm(B[6][0:16, 16 * c:16 * c + 16], T.gt[:, 256 + 16 * c:272 + 16 * c], T.ef[:]) for c in range(4)], g_f, n_e))
+    f_2 = put(N("v", cp(T.zf[0:16, :], B[6][0:16, 0:64]), f_1))
+    f_3 = put(N("p", [mm(B[7][:, 0:32], T.mu[0:16, :], T.zf[0:16, 0:64:2], True, False),
+                      mm(B[7][:, 0:32], T.mu[0:16, :], T.zf[0:16, 1:64:2], False, True)], f_2))
+    f_4 = put(N("v", ts(T.offy[:], B[7][:, 0:32], 128.0, A.add), f_3))
+    y_a = put(N("v", cp(T.yo[:, 0:256], T.xw[:].indirect(T.offy[:, 0:16])), f_4, *ready))
+    y_b = put(N("s", act(T.yo[:, 256:512], T.xw[:].indirect(T.offy[:, 16:32]), F.Identity, -0.0), f_4, *ready))
+    flush()
     wait("y", [y_a])
     g.sync.dma_start(T.y[:, 0:256], T.yo[:, 0:256]).then_inc(sem.dy, 16)
     wait("s", [y_b])

from concourse.bass import DstId, RemoteDMATransfer
from concourse.mybir import AluOpType as A, ActivationFunctionType as F

BF, FL = "bfloat16", "float32"
SCRATCH = {
    "nxs": ("sbuf", [128, 64], "int32"),
    "xw": ("sbuf", [128, 2048], BF),
    "yo": ("sbuf", [128, 512], BF),
    "pi": ("sbuf", [128, 1], "int32"), "vr": ("sbuf", [128, 16], FL),
    "ju": ("sbuf", [128, 128], BF), "jg": ("sbuf", [128, 128], BF), "jq": ("sbuf", [128, 128], BF),
    "jp": ("sbuf", [128, 128], BF), "jw": ("sbuf", [128, 64], BF), "jj": ("sbuf", [128, 256], BF),
    "pc": ("sbuf", [128, 16], "int32"), "pf": ("sbuf", [128, 8], FL), "pd": ("sbuf", [128, 40], FL),
    "kb": ("sbuf", [128, 8], FL), "zo": ("sbuf", [128, 80], BF),
    "l16": ("sbuf", [128, 2], "uint16"), "lz": ("sbuf", [128, 4], "uint16"),
    "i0": ("sbuf", [128, 16], FL), "q3b": ("sbuf", [128, 16], FL),
    "mu": ("sbuf", [128, 128], BF), "mw": ("sbuf", [128, 64], BF), "cs": ("sbuf", [128, 128], BF),
    "bd": ("sbuf", [128, 128], BF), "lx": ("sbuf", [128, 128], BF), "lr": ("sbuf", [128, 128], BF),
    "eye": ("sbuf", [128, 768], BF),
    "bdv": ("sbuf", [128, 512], BF), "ltv": ("sbuf", [128, 512], BF), "lhv": ("sbuf", [128, 512], BF),
    "ck": ("sbuf", [128, 768], BF),
    "lw": ("sbuf", [128, 128], BF), "lwt": ("sbuf", [128, 128], BF), "lwh": ("sbuf", [128, 128], BF),
    "on": ("sbuf", [128, 256], BF),
    "ef": ("sbuf", [128, 16], BF),
    "t0": ("sbuf", [128, 16], "int32"), "h0": ("sbuf", [128, 16], "int32"),
    "e0": ("sbuf", [128, 16], FL), "e1": ("sbuf", [128, 16], BF), "e2": ("sbuf", [128, 16], BF),
    "er": ("sbuf", [128, 16], FL), "hd": ("sbuf", [128, 4], "int32"), "hf": ("sbuf", [128, 1], FL),
    "zt": ("sbuf", [128, 64], BF), "zh": ("sbuf", [128, 64], BF),
    "w0": ("sbuf", [128, 512], BF), "w1": ("sbuf", [128, 512], BF),
    "m": ("sbuf", [128, 320], BF), "gt": ("sbuf", [128, 320], BF), "sc": ("sbuf", [128, 320], FL),
    "off": ("sbuf", [128, 20], "uint16"), "zf": ("sbuf", [128, 64], BF), "offy": ("sbuf", [128, 32], "uint16"),
}
for _k in range(8):
    SCRATCH["b%d" % _k] = ("psum", [128, 512], FL)
SEMAPHORES = ["sv", "ss", "sp", "si", "dn", "dx", "dy", "rl", "an", "ax", "ap"]

SZ, ST = [96, 96, 64], [0, 96, 192]
BX, BW, BR, RO = [0, 1, 2], [3, 6, 7], [3, 4, 5], [96, 0, 0]
ORD = {"v": "g0 o2- oS- g1 g2 c0 c1 o0 e2 o1 c2".split(),
       "s": "m0 e0 e1 m1 m2 mS".split(),
       "p": "x0 r0 w0 x1 w1 w2 x2 r1 r2".split()}


def bits(m):
    return [1 << k for k in range(32) if m >> k & 1]


def shares(core, dests, topo):
    out, used, by, n = {}, 0, {}, 16
    for d in dests:
        by.setdefault(topo.mask(core, d), []).append(d)
    for m in sorted(by, key=lambda v: len(bits(v))):
        free = bits(m & ~used)
        while n * len(by[m]) > len(free):
            n //= 2
        for k, d in enumerate(by[m]):
            out[d] = sum(free[k * n:k * n + n])
            used |= out[d]
    return out


def rank_program(g, core, T, topo):
    rank = T.rank_of(core)
    if rank is None:
        return
    sem = T.sem
    others = [d for d in T.cores if d != core]
    near = [d for d in others if topo.host(d) == topo.host(core) and topo.chip(d) == topo.chip(core)][0]
    peer = [d for d in others if topo.same_plane(core, d) and topo.die(d) == topo.die(core)][0]
    Q = {"v": g.vector, "s": g.scalar, "p": g.tensor, "i": g, "y": g.sync}
    S = {"v": "sv", "s": "ss", "p": "sp", "i": "si"}
    cnt, seen = {}, {}

    def wait(q, deps):
        need = {}
        for d in deps:
            if isinstance(d, dict):
                d = d["tok"]
            need[d[0]] = max(need.get(d[0], 0), d[1])
        for s in sorted(need):
            if seen.get((q, s), 0) < need[s]:
                Q[q].wait_ge(sem[s], need[s])
                seen[(q, s)] = need[s]

    def op(q, call, deps=()):
        wait(q, deps)
        call(Q[q]).then_inc(sem[S[q]], 1)
        cnt[S[q]] = cnt.get(S[q], 0) + 1
        return (S[q], cnt[S[q]])

    lists = {"v": [], "s": [], "p": []}

    def N(q, calls, *deps):
        return {"q": q, "calls": calls if isinstance(calls, list) else [calls], "deps": [d for d in deps if d], "tok": None}

    def put(*nodes):
        for n in nodes:
            lists[n["q"]].append(n)
        return nodes[-1] if nodes else None

    def flush():
        moved = True
        while moved:
            moved = False
            for q in "vps":
                while lists[q] and not any(isinstance(d, dict) and d["tok"] is None for d in lists[q][0]["deps"]):
                    n = lists[q].pop(0)
                    for j, c in enumerate(n["calls"]):
                        n["tok"] = op(q, c, n["deps"] if j == 0 else ())
                    moved = True
        assert not any(lists.values())

    def mm(out, l, r, a=True, z=True):
        return lambda e: e.matmul(out, l, r, a, z)

    def act(out, in_, f, b=0.0, m=1.0):
        return lambda e: e.activation(out, in_, f, bias=b, scale=m)

    def ts(out, in0, s1, o1, s2=None, o2=None):
        if o2 is None:
            return lambda e: e.tensor_scalar(out, in0, s1, None, o1)
        return lambda e: e.tensor_scalar(out, in0, s1, s2, o1, o2)

    def tt(out, a, b, o):
        return lambda e: e.tensor_tensor(out, a, b, o)

    def cp(out, a):
        return lambda e: e.tensor_copy(out, a)

    def scan(out, c, x):
        return lambda e: e.tensor_tensor_scan(out, c, x, 0.0, A.add, A.max)

    def TS(out, in0, s1, o1, s2=None, o2=None, deps=()):
        return op("v", ts(out, in0, s1, o1, s2, o2), deps)

    def LIN(out, a, m, b, *deps):
        return op("s", act(out, a, F.Identity, b, m), deps)

    c0 = 16 * rank
    slot = T.nxs[:, c0:c0 + 16]
    p0 = 32 * rank
    g.sync.dma_start(T.nxs[p0:p0 + 16, c0:c0 + 16], T.nx[:, 0:16]).then_inc(sem.dn, 16)
    g.scalar.dma_start(T.nxs[p0 + 16:p0 + 32, c0:c0 + 16], T.nx[:, 16:32]).then_inc(sem.dn, 16)
    g.sync.dma_start(T.xw[:, 512 * rank:512 * rank + 512], T.x[:, :]).then_inc(sem.dx, 16)
    ms = []
    for a, b in {0: [(32, 64), (64, 128)], 1: [(0, 32), (64, 128)], 2: [(0, 64), (96, 128)], 3: [(0, 64), (64, 96)]}[rank]:
        ms.append(op("v", lambda e: e.memset(T.nxs[a:b, c0:c0 + 16], 0)))

    def IO(out, pat, base=0, cm=0, flag=True):
        if flag:
            return op("i", lambda e: e.iota(out, pat, base, cm, allow_small_or_imprecise_dtypes=True))
        return op("i", lambda e: e.iota(out, pat, base, cm))
    i_p = IO(T.pi[:], [[0, 1]], 0, 1, False)
    i_r = IO(T.vr[:], [[1, 16]])
    i_w = IO(T.jw[:], [[0, 16], [1, 4]])
    i_g = IO(T.jg[:], [[1, 8], [0, 16]])
    i_q = IO(T.jq[:], [[0, 8], [1, 8], [8, 2]])

    sent = [0]

    def send(dests, ap):
        mk, tr = shares(core, [d for d, _ in dests], topo), []
        for d, r_ in dests:
            rid, pid = topo.addr(d, core)
            tr.append(RemoteDMATransfer(dst_ids=[DstId(rid=rid, pnc=pid)], dma_engine_mask=mk[d], remote_sem=r_, src=ap, dst=ap))
            sent[0] += len(bits(mk[d]))
        g.remote_dma_fused(tr, local_sem=sem.rl)

    def part(src, dests, d):
        return len(bits(shares(src, dests, topo)[d]))

    def xs(c):
        r_ = T.rank_of(c)
        return T.xw[:, 512 * r_:512 * r_ + 512]
    wait("i", [("dn", 32)] + ms)
    send([(d, sem.an) for d in others], slot)
    i_u = IO(T.ju[:], [[0, 8], [1, 16]])
    i_y = IO(T.jp[:], [[1, 128]])
    i_j = IO(T.jj[:], [[1, 256]], -128)
    wait("i", [("dx", 16)])
    send([(near, sem.ax), (peer, sem.ap)], xs(core))
    nearpeer = [d for d in others if d not in (near, peer)][0]
    n_an = sum(part(d, [e for e in T.cores if e != d], core) for d in others)
    n_ap = part(peer, [nearpeer, core], core)
    n_ax = part(near, [core, nearpeer], core) + part(near, [core], core)
    ready = [("ax", n_ax), ("ap", n_ap), ("dx", 16)]
    wait("i", [("ap", n_ap)])
    send([(near, sem.ax)], xs(peer))

    pc, pf, pd, kb = T.pc, T.pf, T.pd, T.kb
    SR, AND, EQ = A.logical_shift_right, A.bitwise_and, A.is_equal

    def D(k):
        return pd[:, k:k + 1]

    def of(t, v):
        return t[:, 128 * v:128 * v + 128]
    ca, cb, cc, cd, ce, cf = [of(T.ck, v) for v in range(6)]
    for k, (a, b) in enumerate([(0, 15), (4, 15), (1, 7), (0, 1), (0, 240), (1, 112), (2, 3), (0, 3)]):
        c_ = TS(pc[:, k:k + 1], T.pi[:], a, SR, b, AND, [i_p])
    c_f = op("v", cp(pf[:, 0:8], pc[:, 0:8]), [c_])
    u, gc, q3, ch, uw, uv = pf[:, 0:1], pf[:, 1:2], pf[:, 2:3], pf[:, 3:4], pf[:, 6:7], pf[:, 7:8]
    c_7 = TS(D(7), gc, 7.0, EQ, deps=[c_f])
    TS(T.l16[:, 0:1], pf[:, 5:6], u, A.add)
    TS(T.lz[:], T.vr[:, 0:4], 4.0, A.mult, uw, A.add, [i_r])
    c_b = TS(D(6), D(7), -8.0, A.mult, gc, A.add, [c_7])
    c_v = TS(pd[:, 24:28], T.vr[:, 0:4], uv, EQ)
    TS(T.mw[:], T.jw[:], uw, EQ, deps=[i_w])
    c_b = TS(D(18), D(6), 1.0, A.add, deps=[c_b])
    k_8 = LIN(D(8), D(7), 1.0, -0.5, c_7)
    k_e = LIN(D(14), gc, 1.0, 8.0)
    k_f = LIN(D(15), D(18), 1.0, 8.0, c_b)
    k_g = LIN(D(16), ch, 8.0, D(18))
    k_d = LIN(D(13), ch, 8.0, gc)
    k_5 = LIN(D(5), ch, -1.0, 1.0)
    LIN(D(2), q3, -1.0, 0.5)
    k_b = LIN(D(11), q3, -256.0, 2096128.5)
    k_a = LIN(D(10), pf[:, 4:5], 16.0, u)
    LIN(D(0), u, 512.0, -7552.0)
    k_6 = LIN(D(19), ch, 256.0, 0.0)
    c_d = TS(T.bd[:], T.jg[:], gc, EQ, deps=[i_g])
    TS(cc, T.jq[:], gc, EQ, 0.5, A.mult, [i_q])
    TS(ca, T.jq[:], D(14), EQ, 0.5, A.mult, [k_e])
    c_2 = TS(cd, T.jq[:], D(18), EQ, D(8), A.mult, [k_8, c_b])
    c_1 = TS(cb, T.jq[:], D(15), EQ, D(8), A.mult, [k_f])
    c_h = op("v", tt(T.lwh[:], ca, cb, A.add), [c_1])
    c_t = op("v", tt(T.lwt[:], cc, cd, A.add))
    k_i = LIN(T.i0[:], T.vr[:], 16.0, D(10), i_r, k_a)
    LIN(T.q3b[:], T.vr[:], 0.0, D(11), k_b)
    for dst, src, dep in ((T.bdv, T.bd, c_d), (T.lhv, T.lwh, c_h), (T.ltv, T.lwt, c_t)):
        for v in range(4):
            k_l = LIN(of(dst, v), src[:], D(24 + v), 0.0, c_v, dep)
    op("v", lambda e: e.memset(of(T.on, 0), -1.0))
    op("v", lambda e: e.memset(of(T.on, 1), -256.0))
    TS(D(4), u, 0.0, EQ, -128.0, A.mult)
    TS(ce, T.jq[:], D(13), EQ, 0.5, A.mult, [k_d])
    c_3 = TS(cf, T.jq[:], D(16), EQ, D(8), A.mult, [k_g])
    TS(T.lx[:], T.jg[:], gc, EQ, D(5), A.mult, [k_5])
    TS(T.lr[:], T.jg[:], gc, EQ, ch, A.mult)
    op("v", tt(T.lw[:], ce, cf, A.add), [c_3])
    for k in range(7):
        c_ = TS(pc[:, 8 + k:9 + k], T.pi[:], k, SR, 1, AND)
    op("v", cp(D(28), T.pi[:]))
    op("v", lambda e: e.memset(T.zo[:, 0:64], 0.0))
    op("v", lambda e: e.memset(T.zo[:, 64:80], 1.0))
    n_k = TS(kb[:, 0:7], pc[:, 8:15], -256.0, A.mult, 256.0, A.add, [c_])
    c_u = TS(T.mu[:], T.ju[:], u, EQ, deps=[i_u])
    k_s = LIN(T.cs[:], T.mu[:], -33280.0, 512.0, c_u)
    c_9 = TS(D(9), u, 1.0, EQ, 3.0, A.mult)
    c_3 = TS(D(3), u, 0.0, EQ)
    k_h = LIN(D(17), ch, 0.5, D(9), c_9)
    idw = [LIN(T.w0[:, 256:512], T.jj[:], D(3), D(17), i_j, k_h, c_3)]
    late = [N("v", ts(of(T.eye, k), T.jp[:], D(28), EQ, kb[:, k + 1:k + 2], A.mult), i_y, n_k) for k in range(6)]
    late.append(N("v", ts(T.ef[:, 0:16:2], T.jg[:, 0:128:16], gc, EQ, D(5), A.mult), k_5))
    n_e = N("v", ts(T.ef[:, 1:16:2], T.jg[:, 0:128:16], gc, EQ, D(19), A.mult), k_6)
    late.append(n_e)

    B = [T["b%d" % k] for k in range(8)]
    wait("v", [("dn", 32), ("an", n_an), ("sv", cnt["sv"])])
    nx = T.nxs[:].indirect(T.l16[:, 0:1])
    h_0 = put(N("v", ts(T.h0[:], nx, 8, SR)))
    t_0 = put(N("v", ts(T.t0[:], nx, 255, AND)))
    e_0 = put(N("v", tt(T.e0[:], nx, T.i0[:], A.not_equal), k_i))
    z_h = put(N("v", tt(T.zh[:], T.h0[:].indirect(T.lz[:]), T.mw[:], A.mult), h_0))
    put(N("v", tt(T.e1[:], T.e0[:], T.t0[:], A.mult), e_0))
    e_2 = put(N("v", tt(T.e2[:], T.e0[:], T.h0[:], A.mult)))
    z_t = put(N("v", tt(T.zt[:], T.t0[:].indirect(T.lz[:]), T.mw[:], A.mult), t_0))
    o_t = put(N("v", cp(T.off[:, 0:16], T.t0[:])))
    for v in range(4):
        put(N("p", mm(B[v][:, 0:64], of(T.lhv, v), T.zh[:], True, False), z_h, k_l))
    h_5 = put(N("p", [mm(B[5][:, 0:16], of(T.on, 0), T.e1[:], True, False), mm(B[5][:, 0:16], of(T.on, 1), T.e2[:], False, True)], e_2))
    R = [put(N("p", mm(B[4][:, v:256:4], of(T.bdv, v), T.zh[:]))) for v in range(4)]
    W = [put(N("p", mm(B[v][:, 0:64], of(T.ltv, v), T.zt[:], False, True), z_t)) for v in range(4)]
    h_6 = N("s", lambda e: e.activation(T.er[:], B[5][:, 0:16], F.Copy, accum_out=T.hf[:]), h_5)
    m_a = N("s", act(T.m[:, 0:96], B[4][:, 0:96], F.Sign, D(2)), R[3])
    m_b = N("s", act(T.m[:, 96:256], B[4][:, 96:256], F.Sign, D(2)), R[3])
    m_s = N("s", act(T.m[:, 256:272], T.q3b[:], F.Sign, T.hf[:]), h_6)
    w_ev = [N("v", ts(T.w0[:, v:256:4], B[v][:, 0:64], D(4), A.add), W[v]) if v % 2 == 0 else
            N("s", act(T.w0[:, v:256:4], B[v][:, 0:64], F.Identity, D(4)), W[v]) for v in range(4)]
    idw.append(N("s", act(T.w1[:, 256:512], T.jj[:], F.Identity, D(17), D(3))))
    put(h_6, m_a, w_ev[1], w_ev[3], m_b, m_s, idw[1])
    h_7 = N("v", ts(T.hd[:, 0:1], T.hf[:], 2096128.0, A.add), h_6)
    h_8 = N("v", ts(T.hd[:, 1:2], T.hd[:, 0:1], 255, AND), h_7)
    o_s = N("v", ts(T.off[:, 16:17], T.hd[:, 1:2], kb[:, 0:1], A.add), h_8, n_k)
    put(*late[:6])
    put(h_7, w_ev[0], w_ev[2], h_8)
    put(*late[6:])

    wins = [T.w0, T.w1]
    m_p, o_p, prev = [m_a, m_b, m_b], [o_t, o_t, o_t], {"oS": o_s}
    last = {0: 9, 1: 9, 2: 10, 3: 10}[rank]
    lastsq = 7 if rank == 0 else last - 1
    for k in range(last):
        cur, nxt = wins[k % 2], wins[(k + 1) % 2]
        square = k < lastsq
        ns = {7: 16, 8: 32, 9: 64 if rank == 3 else 0}.get(k, 16)
        so = {7: 17, 8: 18}.get(k, 16)
        nk = ns // 16
        nd, wd = {}, [SZ[0], SZ[1], SZ[2] + (ns if square else 0)]
        if k <= lastsq:
            for i in range(3):
                a, b = ST[i], ST[i] + wd[i]
                seq = [o_s, m_s] + idw if i == 2 and square else []
                nd["g%d" % i] = N("v", tt(T.gt[:, a:b], cur[:].indirect(T.off[:, a // 16:b // 16]), T.m[:, a:b], A.mult),
                                  o_p[i], m_p[i], *(w_ev + seq))
                nd["w%d" % i] = N("p", mm(B[BW[i]][:, 0:SZ[i]], T.lw[:], T.gt[:, a:a + SZ[i]]), nd["g%d" % i])
        if square:
            for i in range(3):
                a, n, gi, wi = ST[i], wd[i], nd["g%d" % i], nd["w%d" % i]
                ab, px, pr, pw = T.gt[:, a:a + n], B[BX[i]][:, 0:n], B[BR[i]], B[BW[i]]
                add = i == 2 and k < 6
                x_ = [mm(px, T.lx[:], ab, True, not add)] + ([mm(px, of(T.eye, k), T.zo[:], False, True)] if add else [])
                nd["x%d" % i] = N("p", x_, gi)
                ri = nd["r%d" % i] = N("p", mm(pr[:, RO[i]:RO[i] + n], T.lr[:], ab), gi)
                both = [ri, wi] if BR[i] == BW[i] else []
                n1 = n if so == 16 else SZ[i]
                m_p[i] = nd["m%d" % i] = N("s", act(T.m[:, a:a + n1], pr[:, RO[i]:RO[i] + n1], F.Sign, D(2)), ri, *both)
                out, in_ = nxt[:, a:a + SZ[i]], pw[:, 0:SZ[i]]
                nd["e%d" % i] = N("v", cp(out, in_), wi) if i == 2 else N("s", act(out, in_, F.Copy), wi, *both)
                ci = nd["c%d" % i] = N("v", scan(T.sc[:, a:a + n], T.cs[:, 0:n], px), nd["x%d" % i], k_s)
                o_p[i] = nd["o%d" % i] = N("v", ts(T.off[:, a // 16:(a + n1) // 16], T.sc[:, a + 15:a + n1:16], D(0), A.add), ci)
            m_s, o_s = m_p[2], o_p[2]
            if so != 16:
                m_s = nd["mS"] = N("s", act(T.m[:, 16 * so:16 * so + ns], B[BR[2]][:, 64:64 + ns], F.Sign, D(2)), ri)
                o_s = nd["oS"] = N("v", ts(T.off[:, so:so + nk], T.sc[:, 256 + 15:256 + ns:16], D(0), A.add), ci)
            w_ev = [nd["e%d" % i] for i in range(3)]
            for q in "vps":
                for nm in ORD[q]:
                    n = prev.get(nm[:-1]) if nm[-1] == "-" else nd.get(nm)
                    if n and n["q"] == q:
                        put(n)
            prev = nd
            continue
        tail = [prev[nm] for nm in ("oS", "o2") if nm in prev]
        prev = {}
        if k == lastsq:
            put(nd["g0"], nd["w0"])
            put(*tail)
            put(nd["g1"], nd["w1"])
        if ns:
            ab = T.gt[:, 256:256 + ns]
            gs = put(N("v", tt(ab, cur[:].indirect(T.off[:, 16:16 + nk]), T.m[:, 256:256 + ns], A.mult), o_s, m_s, *w_ev))
            x_ = put(N("p", mm(B[2][:, 0:ns], T.lx[:], ab), gs))
            r_ = put(N("p", mm(B[5][:, 0:ns], T.lr[:], ab)))
        if k == lastsq:
            put(nd["g2"], nd["w2"])
            w_ev = [put(N("s", act(nxt[:, ST[i]:ST[i] + SZ[i]], B[BW[i]][:, 0:SZ[i]], F.Copy), nd["w%d" % i])) for i in range(3)]
        if ns:
            m_s = put(N("s", act(T.m[:, 16 * so:16 * so + ns], B[5][:, 0:ns], F.Sign, D(2)), r_))
            c_ = put(N("v", scan(T.sc[:, 256:256 + ns], T.cs[:, 0:ns], B[2][:, 0:ns]), x_))
            o_s = put(N("v", ts(T.off[:, so:so + nk], T.sc[:, 256 + 15:256 + ns:16], D(0), A.add), c_))

    win = wins[0][:, 256:512] if rank == 0 else wins[last % 2][:, 0:256]
    g_f = put(N("v", tt(T.gt[:, 256:320], win.indirect(T.off[:, 16:20]), T.m[:, 256:320], A.mult), o_s, m_s, *(w_ev + idw)))
    f_1 = put(N("p", [mm(B[6][0:16, 16 * c:16 * c + 16], T.gt[:, 256 + 16 * c:272 + 16 * c], T.ef[:]) for c in range(4)], g_f, n_e))
    f_2 = put(N("v", cp(T.zf[0:16, :], B[6][0:16, 0:64]), f_1))
    f_3 = put(N("p", [mm(B[7][:, 0:32], T.mu[0:16, :], T.zf[0:16, 0:64:2], True, False),
                      mm(B[7][:, 0:32], T.mu[0:16, :], T.zf[0:16, 1:64:2], False, True)], f_2))
    f_4 = put(N("v", ts(T.offy[:], B[7][:, 0:32], 128.0, A.add), f_3))
    y_a = put(N("v", cp(T.yo[:, 0:256], T.xw[:].indirect(T.offy[:, 0:16])), f_4, *ready))
    y_b = put(N("s", act(T.yo[:, 256:512], T.xw[:].indirect(T.offy[:, 16:32]), F.Identity, -0.0), f_4, *ready))
    flush()
    wait("y", [y_a])
    g.sync.dma_start(T.y[:, 0:256], T.yo[:, 0:256]).then_inc(sem.dy, 16)
    wait("s", [y_b])
    g.scalar.dma_start(T.y[:, 256:512], T.yo[:, 256:512]).then_inc(sem.dy, 16)
    wait("i", [("rl", sent[0]), ("sv", cnt["sv"]), ("ss", cnt["ss"]), ("sp", cnt["sp"]), ("dy", 32)])
    wait("v", [("si", cnt["si"])])
